import numpy as np
import ml_dtypes


def mxq(x, axis, fmt="e4m3"):
    dtype, down = {"e4m3": (ml_dtypes.float8_e4m3fn, 7), "e5m2": (ml_dtypes.float8_e5m2, 14)}[fmt]
    v = np.moveaxis(np.asarray(x, np.float32).astype(ml_dtypes.bfloat16).astype(np.float64), axis, -1)
    blocks = v.reshape(v.shape[:-1] + (-1, 32))
    amax = np.abs(blocks).max(-1, keepdims=True)
    byte = np.maximum(np.where(amax > 0, np.frexp(amax)[1] - 1 + 127, 0) - down, 1)
    scale = np.exp2(byte - 127.0)
    codes = (blocks / scale).astype(np.float32).astype(dtype).astype(np.float64)
    return np.moveaxis((codes * scale).reshape(v.shape), -1, axis)


WIDE = False


def mx_kscale(k):
    if not WIDE:
        return np.ones(k)
    levels = np.array([10, -10, 5, -5, 0])
    if k % 512:
        return np.exp2(np.random.permutation(np.resize(levels, k // 32))).repeat(32)
    a = np.empty((k // 512, 16))
    for p in range(k // 512):
        a[p, :8] = np.random.permutation(np.resize(levels, 8))
        for g in range(8):
            far = levels[np.abs(levels - a[p, g]) >= 10]
            a[p, g + 8] = far[np.random.randint(len(far))]
    return np.exp2(a.ravel()).repeat(32)


def f64(x):
    return np.asarray(x).astype(np.float64)


def striped(idx):
    return np.tile(idx.reshape(-1, 16).T, (8, 1)).astype(np.uint16)


def unstriped(offs):
    return offs[:16].T.reshape(-1).astype(np.int64)


def pack_weight(w):
    k, n = w.shape
    w = f64(np.asarray(w, np.float32).astype(ml_dtypes.bfloat16)).reshape(k // 32, 32, n)
    amax = np.abs(w).max(1)
    byte = np.clip(np.where(amax > 0, np.frexp(amax)[1] - 1 + 127 - 7, 1), 1, 254)
    scaled = (w * np.exp2(127.0 - byte)[:, None, :]).reshape(k, n).astype(np.float32)
    words = np.ascontiguousarray(scaled.reshape(k // 512, 128, 4, n).transpose(0, 1, 3, 2)).astype(ml_dtypes.float8_e4m3fn).view(np.uint8)
    return words, np.ascontiguousarray(byte.astype(np.uint8).reshape(k // 512, 16, n))


def unpack_weight(words, scales):
    g, p, n, _ = words.shape
    vals = np.ascontiguousarray(words).view(ml_dtypes.float8_e4m3fn).astype(np.float64) * np.repeat(np.exp2(scales.astype(np.float64) - 127.0), 8, axis=1)[..., None]
    return vals.transpose(0, 1, 3, 2).reshape(g * 512, n)


def relu(v):
    return np.maximum(v, 0.0)


K, T, S, H, N, U = 1024, 2048, 1024, 512, 256, 1024


def setup_inputs():
    n = np.random.standard_normal
    s = mx_kscale(K)[:, None]
    u = mx_kscale(H)
    packed_xT = pack_weight(n((K, T)) * s)
    packed_w3 = pack_weight(n((H, N)) / np.sqrt(H) / u[:, None])
    return {
        "x_words": packed_xT[0],
        "x_scales": packed_xT[1],
        "w1": (n((K, H)) / np.sqrt(2 * K) / s * u).astype(np.float32),
        "w2": (n((K, H)) / np.sqrt(2 * K) / s * u).astype(np.float32),
        "w3_words": packed_w3[0],
        "w3_scales": packed_w3[1],
        "offs": striped(np.random.permutation(T)[:S]),
        "src": striped(np.random.permutation(S)[(S * np.random.uniform(0, 1, U) ** 4).astype(np.int64)]),
        "dst": striped(np.random.permutation(S)),
    }


def reference(x_words, x_scales, w1, w2, w3_words, w3_scales, offs, src, dst):
    xq = unpack_weight(x_words, x_scales)[:, unstriped(offs)]
    y = mxq(f64(w1), 0, "e4m3").T @ xq
    e = mxq(f64(w2), 0, "e4m3").T @ xq
    z = relu(y[:, unstriped(src)] + e[:, unstriped(dst)])
    return unpack_weight(w3_words, w3_scales).T @ mxq(z, 0, "e4m3")

@@ -1,0 +1,213 @@
+from contextlib import ExitStack
+
+import concourse.mybir as mybir
+
+K, T, S, H, N = 1024, 2048, 1024, 512, 256
+FLOPS = 2 * (2 * K * H * S + H * N * S)
+
+F32 = mybir.dt.float32
+BF16 = mybir.dt.bfloat16
+I32 = mybir.dt.int32
+U32 = mybir.dt.uint32
+U16 = mybir.dt.uint16
+U8 = mybir.dt.uint8
+FP8X4 = mybir.dt.float8_e4m3fn_x4
+ACT = mybir.ActivationFunctionType
+ALU = mybir.AluOpType
+
+P = 128
+PACK = 4
+K_PASS = P * PACK
+PASSES = K // K_PASS
+BANK = 512
+HALVES = S // BANK
+STRIPE = 16
+EDGE_CHUNKS = (256, 256, 256, 128, 128)
+
+
+def tile_picked_hub_relu_p_kernel(
+    tc, x_words, x_scales, w1, w2, w3_words, w3_scales, offs, src, dst, out
+):
+    nc = tc.nc
+    with ExitStack() as ctx:
+        keep = ctx.enter_context(tc.tile_pool(name="keep", bufs=1))
+        acc_pool = ctx.enter_context(tc.psum_pool(name="acc", bufs=6))
+        out_pool = ctx.enter_context(tc.psum_pool(name="outp", bufs=2))
+
+        def entries(list_tile, first, count):
+            return list_tile[:, first // STRIPE : (first + count) // STRIPE]
+
+        offs_sb = keep.tile([P, S // STRIPE], U16, name="offs_sb")
+        src_sb = keep.tile([P, S // STRIPE], U16, name="src_sb")
+        dst_sb = keep.tile([P, S // STRIPE], U16, name="dst_sb")
+        nc.sync.dma_start(offs_sb[:], offs)
+
+        xs_all = keep.tile([P, T], U8, name="xs_all", align_bytes=64)
+        nc.vector.memset(xs_all[:].bitcast(I32), 0)
+        xs_rows = keep.tile([P, T // 4], I32, name="xs_rows")
+        for q in range(4):
+            rows = slice(32 * q, 32 * q + 4 * PASSES)
+            nc.sync.dma_start(xs_rows[rows, :], x_scales[:, 4 * q : 4 * q + 4, :].bitcast(I32))
+            nc.vector.tensor_copy(xs_all[rows, :].bitcast(I32), xs_rows[rows, :])
+
+        xw_all = [keep.tile([P, T], I32, name=f"xw_all{g}", align_bytes=64) for g in range(PASSES)]
+
+        def load_x(g):
+            nc.sync.dma_start(xw_all[g][:], x_words[g].rearrange("p n t -> p (n t)").bitcast(I32))
+
+        def load_w(w, name, g, c0, c1):
+            raw = keep.tile([P, PACK, c1 - c0], F32, name=f"{name}_raw{g}_{c0}")
+            rows = w[g * K_PASS : (g + 1) * K_PASS, c0:c1]
+            nc.sync.dma_start(raw[:], rows.rearrange("(p j) c -> p j c", j=PACK))
+            return raw
+
+        w1_raw0 = [load_w(w1, "w1", 0, c0, c0 + H // 2) for c0 in (0, H // 2)]
+        load_x(0)
+        load_x(1)
+        w1_raw1 = [load_w(w1, "w1", 1, c0, c0 + H // 2) for c0 in (0, H // 2)]
+        nc.sync.dma_start(src_sb[:], src)
+        w2_raw = [[load_w(w2, "w2", g, c0, c0 + H // 2) for c0 in (0, H // 2)] for g in range(PASSES)]
+        nc.sync.dma_start(dst_sb[:], dst)
+        w3_codes = keep.tile([P, N], I32, name="w3_codes", align_bytes=64)
+        nc.sync.dma_start(w3_codes[:], w3_words[0].rearrange("p n t -> p (n t)").bitcast(I32))
+        w3_sc = keep.tile([P, N], U8, name="w3_sc", align_bytes=64)
+        nc.vector.memset(w3_sc[:].bitcast(I32), 0)
+        for q in range(4):
+            nc.sync.dma_start(
+                w3_sc[32 * q : 32 * q + 4, :].bitcast(I32), w3_scales[0, 4 * q : 4 * q + 4, :].bitcast(I32)
+            )
+
+        xw = [keep.tile([P, S], U32, name=f"xw{g}", align_bytes=64) for g in range(PASSES)]
+        xs = keep.tile([P, S], U8, name="xs", align_bytes=64)
+        nc.vector.tensor_copy(xs[:], xs_all[:].indirect(offs_sb[:]))
+
+        def weight_tiles(name, g):
+            dealt = keep.tile([P, PACK, P, PACK], BF16, name=f"{name}_bf{g}", align_bytes=64)
+            codes = keep.tile([P, H], U32, name=f"{name}_codes{g}", align_bytes=64)
+            scales = keep.tile([P, H], U8, name=f"{name}_scales{g}", align_bytes=64)
+            return dealt, codes, scales
+
+        def deal_views(dealt, raw, c0):
+            m0, m1 = c0 // PACK, (c0 + raw.shape[2]) // PACK
+            return (
+                dealt[:, :, m0:m1, :].rearrange("p t m j -> p m j t"),
+                raw[:].rearrange("p j (m t) -> p m j t", t=PACK),
+            )
+
+        def quantise_weights(tiles, t0, t1):
+            dealt, codes, scales = tiles
+            nc.vector.quantize_mx(
+                out=codes[:, t0 * P : t1 * P].bitcast(FP8X4),
+                scales=scales[:, t0 * P : t1 * P],
+                in_=dealt[:, t0:t1, :, :].rearrange("p t m j -> p (t m j)"),
+            )
+
+        def product(w_tiles, name, t, second_engine):
+            res = keep.tile([P, S], F32, name=f"{name}{t}")
+            for h in range(HALVES):
+                cols = slice(h * BANK, (h + 1) * BANK)
+                acc = acc_pool.tile([P, BANK], F32, name="acc")
+                for g in range(PASSES):
+                    nc.tensor.matmul_mx(
+                        out=acc[:],
+                        lhsT=w_tiles[g][1][:, t * P : (t + 1) * P].bitcast(FP8X4),
+                        lhsT_scale=w_tiles[g][2][:, t * P : (t + 1) * P],
+                        rhs=xw[g][:, cols].bitcast(FP8X4),
+                        rhs_scale=xs[4 * g :, cols],
+                        start=(g == 0),
+                        stop=(g == PASSES - 1),
+                    )
+                if h == 1 and second_engine:
+                    nc.vector.tensor_copy(res[:, cols], acc[:])
+                else:
+                    nc.scalar.copy(res[:, cols], acc[:])
+            return res
+
+        w1_q = [weight_tiles("w1", g) for g in range(PASSES)]
+        w2_q = [weight_tiles("w2", g) for g in range(PASSES)]
+        for c in range(2):
+            nc.scalar.activation(*deal_views(w1_q[0][0], w1_raw0[c], c * H // 2), ACT.Copy)
+        quantise_weights(w1_q[0], 0, PACK)
+        nc.vector.tensor_copy(xw[0][:], xw_all[0][:].bitcast(U32).indirect(offs_sb[:]))
+        for h in range(HALVES):
+            nc.vector.tensor_copy(
+                xw[1][:, h * BANK : (h + 1) * BANK],
+                xw_all[1][:].bitcast(U32).indirect(entries(offs_sb, h * BANK, BANK)),
+            )
+        nc.scalar.activation(*deal_views(w1_q[1][0], w1_raw1[0], 0), ACT.Copy)
+        nc.vector.tensor_copy(*deal_views(w1_q[1][0], w1_raw1[1], H // 2))
+        for t in range(PACK):
+            quantise_weights(w1_q[1], t, t + 1)
+
+        def fetch_sources(y_t, t):
+            got = []
+            for h in range(HALVES):
+                half = keep.tile([P, BANK], F32, name=f"ysrc{t}_{h}", tag=f"ysrc{t}_{h}", align_bytes=64)
+                nc.vector.tensor_copy(half[:], y_t[:].indirect(entries(src_sb, h * BANK, BANK)))
+                got.append(half)
+            return got
+
+        def deal_w2(piece, engine):
+            g, c = divmod(piece, 2)
+            dealt, raw = deal_views(w2_q[g][0], w2_raw[g][c], c * H // 2)
+            if engine == "s":
+                nc.scalar.activation(dealt, raw, ACT.Copy)
+            elif engine == "v":
+                nc.vector.tensor_copy(dealt, raw)
+            else:
+                nc.gpsimd.tensor_scalar(dealt, raw, 1.0, 0.0, ALU.mult, ALU.add)
+
+        y_src = []
+        y_src.append(fetch_sources(product(w1_q, "y", 0, True), 0))
+        y_src.append(fetch_sources(product(w1_q, "y", 1, False), 1))
+        deal_w2(0, "s")
+        deal_w2(1, "s")
+        quantise_weights(w2_q[0], 0, PACK)
+        y_src.append(fetch_sources(product(w1_q, "y", 2, False), 2))
+        deal_w2(2, "s")
+        deal_w2(3, "s")
+        for u in range(PACK):
+            quantise_weights(w2_q[1], u, u + 1)
+        y_src.append(fetch_sources(product(w1_q, "y", 3, False), 3))
+
+        e = [product(w2_q, "e", t, False) for t in range(PACK)]
+
+        out_rows = out.rearrange("(h p) r -> p h r", p=P)
+        r0 = 0
+        for c, n in enumerate(EDGE_CHUNKS):
+            cols = slice(r0, r0 + n)
+            pre_tag = f"z_bf{c - 3}" if c >= 3 else ("ysrc2_0" if c == 2 else f"pre{c}")
+            pre = keep.tile([P, PACK, n], F32, name=f"pre{c}", tag=pre_tag, align_bytes=64)
+            for t in range(PACK):
+                nc.vector.tensor_tensor(
+                    pre[:, t, :], e[t][:].indirect(entries(dst_sb, r0, n)), y_src[t][r0 // BANK][:, r0 % BANK : r0 % BANK + n], ALU.add
+                )
+            z_bf = keep.tile([P, n, PACK], BF16, name=f"z_bf{c}", tag=f"z_bf{c}", align_bytes=64)
+            nc.scalar.activation(
+                z_bf[:].rearrange("p (a i) t -> p a t i", i=4),
+                pre[:].rearrange("p t (a i) -> p a t i", i=4),
+                ACT.Relu,
+            )
+            z_codes = keep.tile([P, n], U32, name=f"z_codes{c}", align_bytes=64)
+            z_scales = keep.tile([P, n], U8, name=f"z_scales{c}", align_bytes=64)
+            nc.vector.quantize_mx(
+                out=z_codes[:].bitcast(FP8X4), scales=z_scales[:], in_=z_bf[:].rearrange("p r t -> p (r t)")
+            )
+            staged = keep.tile([P, N // P, n], F32, name=f"staged{c}")
+            per_bank = min(N // P, BANK // n)
+            for b in range(0, N // P, per_bank):
+                bank = out_pool.tile([P, per_bank, n], F32, name="bank")
+                for k in range(per_bank):
+                    m_cols = slice((b + k) * P, (b + k + 1) * P)
+                    nc.tensor.matmul_mx(
+                        out=bank[:, k, :],
+                        lhsT=w3_codes[:, m_cols].bitcast(FP8X4),
+                        lhsT_scale=w3_sc[:, m_cols],
+                        rhs=z_codes[:].bitcast(FP8X4),
+                        rhs_scale=z_scales[:],
+                        start=True,
+                        stop=True,
+                    )
+                nc.scalar.copy(staged[:, b : b + per_bank, :], bank[:])
+            nc.sync.dma_start(out_rows[:, :, cols], staged[:])
+            r0 = r0 + n

@@ -31,8 +31,7 @@ def tile_picked_hub_relu_p_kernel(
     nc = tc.nc
     with ExitStack() as ctx:
         keep = ctx.enter_context(tc.tile_pool(name="keep", bufs=1))
-        acc_pool = ctx.enter_context(tc.psum_pool(name="acc", bufs=6))
-        out_pool = ctx.enter_context(tc.psum_pool(name="outp", bufs=2))
+        acc_pool = ctx.enter_context(tc.psum_pool(name="acc", bufs=8))
 
         def entries(list_tile, first, count):
             return list_tile[:, first // STRIPE : (first + count) // STRIPE]
@@ -61,12 +60,12 @@ def tile_picked_hub_relu_p_kernel(
             nc.sync.dma_start(raw[:], rows.rearrange("(p j) c -> p j c", j=PACK))
             return raw
 
-        w1_raw0 = [load_w(w1, "w1", 0, c0, c0 + H // 2) for c0 in (0, H // 2)]
+        w1_raw0 = load_w(w1, "w1", 0, 0, H)
         load_x(0)
         load_x(1)
-        w1_raw1 = [load_w(w1, "w1", 1, c0, c0 + H // 2) for c0 in (0, H // 2)]
+        w1_raw1 = load_w(w1, "w1", 1, 0, H)
         nc.sync.dma_start(src_sb[:], src)
-        w2_raw = [[load_w(w2, "w2", g, c0, c0 + H // 2) for c0 in (0, H // 2)] for g in range(PASSES)]
+        w2_raw = [load_w(w2, "w2", g, 0, H) for g in range(PASSES)]
         nc.sync.dma_start(dst_sb[:], dst)
         w3_codes = keep.tile([P, N], I32, name="w3_codes", align_bytes=64)
         nc.sync.dma_start(w3_codes[:], w3_words[0].rearrange("p n t -> p (n t)").bitcast(I32))
@@ -87,11 +86,11 @@ def tile_picked_hub_relu_p_kernel(
             scales = keep.tile([P, H], U8, name=f"{name}_scales{g}", align_bytes=64)
             return dealt, codes, scales
 
-        def deal_views(dealt, raw, c0):
-            m0, m1 = c0 // PACK, (c0 + raw.shape[2]) // PACK
+        def deal_views(dealt, raw, c0, c1):
+            m0, m1 = c0 // PACK, c1 // PACK
             return (
                 dealt[:, :, m0:m1, :].rearrange("p t m j -> p m j t"),
-                raw[:].rearrange("p j (m t) -> p m j t", t=PACK),
+                raw[:, :, c0:c1].rearrange("p j (m t) -> p m j t", t=PACK),
             )
 
         def quantise_weights(tiles, t0, t1):
@@ -106,7 +105,7 @@ def tile_picked_hub_relu_p_kernel(
             res = keep.tile([P, S], F32, name=f"{name}{t}")
             for h in range(HALVES):
                 cols = slice(h * BANK, (h + 1) * BANK)
-                acc = acc_pool.tile([P, BANK], F32, name="acc")
+                acc = acc_pool.tile([P, BANK], F32, name="acc", tag="acc")
                 for g in range(PASSES):
                     nc.tensor.matmul_mx(
                         out=acc[:],
@@ -125,8 +124,8 @@ def tile_picked_hub_relu_p_kernel(
 
         w1_q = [weight_tiles("w1", g) for g in range(PASSES)]
         w2_q = [weight_tiles("w2", g) for g in range(PASSES)]
-        for c in range(2):
-            nc.scalar.activation(*deal_views(w1_q[0][0], w1_raw0[c], c * H // 2), ACT.Copy)
+        nc.scalar.activation(*deal_views(w1_q[0][0], w1_raw0, 0, H // 2), ACT.Copy)
+        nc.vector.tensor_copy(*deal_views(w1_q[0][0], w1_raw0, H // 2, H))
         quantise_weights(w1_q[0], 0, PACK)
         nc.vector.tensor_copy(xw[0][:], xw_all[0][:].bitcast(U32).indirect(offs_sb[:]))
         for h in range(HALVES):
@@ -134,8 +133,8 @@ def tile_picked_hub_relu_p_kernel(
                 xw[1][:, h * BANK : (h + 1) * BANK],
                 xw_all[1][:].bitcast(U32).indirect(entries(offs_sb, h * BANK, BANK)),
             )
-        nc.scalar.activation(*deal_views(w1_q[1][0], w1_raw1[0], 0), ACT.Copy)
-        nc.vector.tensor_copy(*deal_views(w1_q[1][0], w1_raw1[1], H // 2))
+        nc.scalar.activation(*deal_views(w1_q[1][0], w1_raw1, 0, 192), ACT.Copy)
+        nc.vector.tensor_copy(*deal_views(w1_q[1][0], w1_raw1, 192, H))
         for t in range(PACK):
             quantise_weights(w1_q[1], t, t + 1)
 
@@ -149,7 +148,7 @@ def tile_picked_hub_relu_p_kernel(
 
         def deal_w2(piece, engine):
             g, c = divmod(piece, 2)
-            dealt, raw = deal_views(w2_q[g][0], w2_raw[g][c], c * H // 2)
+            dealt, raw = deal_views(w2_q[g][0], w2_raw[g], c * H // 2, (c + 1) * H // 2)
             if engine == "s":
                 nc.scalar.activation(dealt, raw, ACT.Copy)
             elif engine == "v":
@@ -183,11 +182,12 @@ def tile_picked_hub_relu_p_kernel(
                     pre[:, t, :], e[t][:].indirect(entries(dst_sb, r0, n)), y_src[t][r0 // BANK][:, r0 % BANK : r0 % BANK + n], ALU.add
                 )
             z_bf = keep.tile([P, n, PACK], BF16, name=f"z_bf{c}", tag=f"z_bf{c}", align_bytes=64)
-            nc.scalar.activation(
-                z_bf[:].rearrange("p (a i) t -> p a t i", i=4),
-                pre[:].rearrange("p t (a i) -> p a t i", i=4),
-                ACT.Relu,
-            )
+            woven = z_bf[:].rearrange("p (a i) t -> p a t i", i=4)
+            planes = pre[:].rearrange("p t (a i) -> p a t i", i=4)
+            if c + 1 < len(EDGE_CHUNKS):
+                nc.scalar.activation(woven, planes, ACT.Relu)
+            else:
+                nc.vector.tensor_scalar_max(woven, planes, 0.0)
             z_codes = keep.tile([P, n], U32, name=f"z_codes{c}", align_bytes=64)
             z_scales = keep.tile([P, n], U8, name=f"z_scales{c}", align_bytes=64)
             nc.vector.quantize_mx(
@@ -196,7 +196,7 @@ def tile_picked_hub_relu_p_kernel(
             staged = keep.tile([P, N // P, n], F32, name=f"staged{c}")
             per_bank = min(N // P, BANK // n)
             for b in range(0, N // P, per_bank):
-                bank = out_pool.tile([P, per_bank, n], F32, name="bank")
+                bank = acc_pool.tile([P, per_bank, n], F32, name="bank", tag="acc")
                 for k in range(per_bank):
                     m_cols = slice((b + k) * P, (b + k + 1) * P)
                     nc.tensor.matmul_mx(

@@ -86,11 +86,11 @@ def tile_picked_hub_relu_p_kernel(
             scales = keep.tile([P, H], U8, name=f"{name}_scales{g}", align_bytes=64)
             return dealt, codes, scales
 
-        def deal_views(dealt, raw, c0, c1):
+        def deal_views(dealt, raw, c0, c1, walk="m j t"):
             m0, m1 = c0 // PACK, c1 // PACK
             return (
-                dealt[:, :, m0:m1, :].rearrange("p t m j -> p m j t"),
-                raw[:, :, c0:c1].rearrange("p j (m t) -> p m j t", t=PACK),
+                dealt[:, :, m0:m1, :].rearrange(f"p t m j -> p {walk}"),
+                raw[:, :, c0:c1].rearrange(f"p j (m t) -> p {walk}", t=PACK),
             )
 
         def quantise_weights(tiles, t0, t1):
@@ -103,9 +103,10 @@ def tile_picked_hub_relu_p_kernel(
 
         def product(w_tiles, name, t, second_engine):
             res = keep.tile([P, S], F32, name=f"{name}{t}")
-            for h in range(HALVES):
-                cols = slice(h * BANK, (h + 1) * BANK)
-                acc = acc_pool.tile([P, BANK], F32, name="acc", tag="acc")
+            width = BANK // 2 if second_engine else BANK
+            for h in range(S // width):
+                cols = slice(h * width, (h + 1) * width)
+                acc = acc_pool.tile([P, width], F32, name="acc", tag="acc")
                 for g in range(PASSES):
                     nc.tensor.matmul_mx(
                         out=acc[:],
@@ -116,7 +117,7 @@ def tile_picked_hub_relu_p_kernel(
                         start=(g == 0),
                         stop=(g == PASSES - 1),
                     )
-                if h == 1 and second_engine:
+                if h % 2 == 1 and second_engine:
                     nc.vector.tensor_copy(res[:, cols], acc[:])
                 else:
                     nc.scalar.copy(res[:, cols], acc[:])
@@ -125,7 +126,7 @@ def tile_picked_hub_relu_p_kernel(
         w1_q = [weight_tiles("w1", g) for g in range(PASSES)]
         w2_q = [weight_tiles("w2", g) for g in range(PASSES)]
         nc.scalar.activation(*deal_views(w1_q[0][0], w1_raw0, 0, H // 2), ACT.Copy)
-        nc.vector.tensor_copy(*deal_views(w1_q[0][0], w1_raw0, H // 2, H))
+        nc.vector.tensor_copy(*deal_views(w1_q[0][0], w1_raw0, H // 2, H, "m t j"))
         quantise_weights(w1_q[0], 0, PACK)
         nc.vector.tensor_copy(xw[0][:], xw_all[0][:].bitcast(U32).indirect(offs_sb[:]))
         for h in range(HALVES):
@@ -134,7 +135,7 @@ def tile_picked_hub_relu_p_kernel(
                 xw_all[1][:].bitcast(U32).indirect(entries(offs_sb, h * BANK, BANK)),
             )
         nc.scalar.activation(*deal_views(w1_q[1][0], w1_raw1, 0, 192), ACT.Copy)
-        nc.vector.tensor_copy(*deal_views(w1_q[1][0], w1_raw1, 192, H))
+        nc.vector.tensor_copy(*deal_views(w1_q[1][0], w1_raw1, 192, H, "m t j"))
         for t in range(PACK):
             quantise_weights(w1_q[1], t, t + 1)
 
@@ -194,7 +195,8 @@ def tile_picked_hub_relu_p_kernel(
                 out=z_codes[:].bitcast(FP8X4), scales=z_scales[:], in_=z_bf[:].rearrange("p r t -> p (r t)")
             )
             staged = keep.tile([P, N // P, n], F32, name=f"staged{c}")
-            per_bank = min(N // P, BANK // n)
+            last = c + 1 == len(EDGE_CHUNKS)
+            per_bank = 1 if last else N // P
             for b in range(0, N // P, per_bank):
                 bank = acc_pool.tile([P, per_bank, n], F32, name="bank", tag="acc")
                 for k in range(per_bank):
@@ -208,6 +210,9 @@ def tile_picked_hub_relu_p_kernel(
                         start=True,
                         stop=True,
                     )
-                nc.scalar.copy(staged[:, b : b + per_bank, :], bank[:])
+                if b == 1:
+                    nc.vector.tensor_copy(staged[:, b : b + per_bank, :], bank[:])
+                else:
+                    nc.scalar.copy(staged[:, b : b + per_bank, :], bank[:])
             nc.sync.dma_start(out_rows[:, :, cols], staged[:])
             r0 = r0 + n

@@ -22,7 +22,7 @@ PASSES = K // K_PASS
 BANK = 512
 HALVES = S // BANK
 STRIPE = 16
-EDGE_CHUNKS = (256, 256, 256, 128, 128)
+EDGE_CHUNKS = ((256, 256), (256, 128), (128,))
 
 
 def tile_picked_hub_relu_p_kernel(
@@ -126,16 +126,12 @@ def tile_picked_hub_relu_p_kernel(
         w1_q = [weight_tiles("w1", g) for g in range(PASSES)]
         w2_q = [weight_tiles("w2", g) for g in range(PASSES)]
         nc.scalar.activation(*deal_views(w1_q[0][0], w1_raw0, 0, H // 2), ACT.Copy)
-        nc.vector.tensor_copy(*deal_views(w1_q[0][0], w1_raw0, H // 2, H, "m t j"))
+        nc.vector.tensor_copy(*deal_views(w1_q[0][0], w1_raw0, H // 2, H))
         quantise_weights(w1_q[0], 0, PACK)
         nc.vector.tensor_copy(xw[0][:], xw_all[0][:].bitcast(U32).indirect(offs_sb[:]))
-        for h in range(HALVES):
-            nc.vector.tensor_copy(
-                xw[1][:, h * BANK : (h + 1) * BANK],
-                xw_all[1][:].bitcast(U32).indirect(entries(offs_sb, h * BANK, BANK)),
-            )
+        nc.vector.tensor_copy(xw[1][:], xw_all[1][:].bitcast(U32).indirect(offs_sb[:]))
         nc.scalar.activation(*deal_views(w1_q[1][0], w1_raw1, 0, 192), ACT.Copy)
-        nc.vector.tensor_copy(*deal_views(w1_q[1][0], w1_raw1, 192, H, "m t j"))
+        nc.vector.tensor_copy(*deal_views(w1_q[1][0], w1_raw1, 192, H))
         for t in range(PACK):
             quantise_weights(w1_q[1], t, t + 1)
 
@@ -173,29 +169,14 @@ def tile_picked_hub_relu_p_kernel(
         e = [product(w2_q, "e", t, False) for t in range(PACK)]
 
         out_rows = out.rearrange("(h p) r -> p h r", p=P)
-        r0 = 0
-        for c, n in enumerate(EDGE_CHUNKS):
-            cols = slice(r0, r0 + n)
-            pre_tag = f"z_bf{c - 3}" if c >= 3 else ("ysrc2_0" if c == 2 else f"pre{c}")
-            pre = keep.tile([P, PACK, n], F32, name=f"pre{c}", tag=pre_tag, align_bytes=64)
-            for t in range(PACK):
-                nc.vector.tensor_tensor(
-                    pre[:, t, :], e[t][:].indirect(entries(dst_sb, r0, n)), y_src[t][r0 // BANK][:, r0 % BANK : r0 % BANK + n], ALU.add
-                )
-            z_bf = keep.tile([P, n, PACK], BF16, name=f"z_bf{c}", tag=f"z_bf{c}", align_bytes=64)
-            woven = z_bf[:].rearrange("p (a i) t -> p a t i", i=4)
-            planes = pre[:].rearrange("p t (a i) -> p a t i", i=4)
-            if c + 1 < len(EDGE_CHUNKS):
-                nc.scalar.activation(woven, planes, ACT.Relu)
-            else:
-                nc.vector.tensor_scalar_max(woven, planes, 0.0)
-            z_codes = keep.tile([P, n], U32, name=f"z_codes{c}", align_bytes=64)
-            z_scales = keep.tile([P, n], U8, name=f"z_scales{c}", align_bytes=64)
+
+        def finish(z_bf, r0, n, last):
+            z_codes = keep.tile([P, n], U32, name=f"z_codes{r0}", align_bytes=64)
+            z_scales = keep.tile([P, n], U8, name=f"z_scales{r0}", align_bytes=64)
             nc.vector.quantize_mx(
                 out=z_codes[:].bitcast(FP8X4), scales=z_scales[:], in_=z_bf[:].rearrange("p r t -> p (r t)")
             )
-            staged = keep.tile([P, N // P, n], F32, name=f"staged{c}")
-            last = c + 1 == len(EDGE_CHUNKS)
+            staged = keep.tile([P, N // P, n], F32, name=f"staged{r0}")
             per_bank = 1 if last else N // P
             for b in range(0, N // P, per_bank):
                 bank = acc_pool.tile([P, per_bank, n], F32, name="bank", tag="acc")
@@ -214,5 +195,36 @@ def tile_picked_hub_relu_p_kernel(
                     nc.vector.tensor_copy(staged[:, b : b + per_bank, :], bank[:])
                 else:
                     nc.scalar.copy(staged[:, b : b + per_bank, :], bank[:])
-            nc.sync.dma_start(out_rows[:, :, cols], staged[:])
-            r0 = r0 + n
+            nc.sync.dma_start(out_rows[:, :, r0 : r0 + n], staged[:])
+
+        r0 = 0
+        pending = []
+        for c, pieces in enumerate(EDGE_CHUNKS):
+            n = sum(pieces)
+            last = c + 1 == len(EDGE_CHUNKS)
+            pre = keep.tile([P, PACK, n], F32, name=f"pre{c}", tag=("pre0", "ysrc2_0", "z_bf256")[c], align_bytes=64)
+            for t in range(PACK):
+                nc.vector.tensor_tensor(
+                    pre[:, t, :],
+                    e[t][:].indirect(entries(dst_sb, r0, n)),
+                    y_src[t][r0 // BANK][:, r0 % BANK : r0 % BANK + n],
+                    ALU.add,
+                )
+            made = []
+            first = 0
+            for width in pieces:
+                z_bf = keep.tile([P, width, PACK], BF16, name=f"z_bf{r0}", tag=f"z_bf{r0}", align_bytes=64)
+                woven = z_bf[:].rearrange("p (a i) t -> p a t i", i=4)
+                planes = pre[:, :, first : first + width].rearrange("p t (a i) -> p a t i", i=4)
+                if last:
+                    nc.vector.tensor_scalar_max(woven, planes, 0.0)
+                else:
+                    nc.scalar.activation(woven, planes, ACT.Relu)
+                made.append((z_bf, r0, width, last))
+                first = first + width
+                r0 = r0 + width
+            for job in pending:
+                finish(*job)
+            pending = made
+        for job in pending:
+            finish(*job)

@@ -19,9 +19,19 @@ P = 128
 PACK = 4
 K_PASS = P * PACK
 PASSES = K // K_PASS
+QUADRANTS = 4
+QUADRANT = P // QUADRANTS
+SCALE_ROWS = 4
 BANK = 512
-HALVES = S // BANK
 STRIPE = 16
+LINE = 4
+
+Y_WINDOW = 1408
+
+W1_LAST_ON_SCALAR = 192
+
+W2_FIRST_ON_VECTOR = 192
+
 EDGE_CHUNKS = ((256, 256), (256, 128), (128,))
 
 
@@ -31,7 +41,7 @@ def tile_picked_hub_relu_p_kernel(
     nc = tc.nc
     with ExitStack() as ctx:
         keep = ctx.enter_context(tc.tile_pool(name="keep", bufs=1))
-        acc_pool = ctx.enter_context(tc.psum_pool(name="acc", bufs=8))
+        psum = ctx.enter_context(tc.psum_pool(name="psum", bufs=8))
 
         def entries(list_tile, first, count):
             return list_tile[:, first // STRIPE : (first + count) // STRIPE]
@@ -43,37 +53,39 @@ def tile_picked_hub_relu_p_kernel(
 
         xs_all = keep.tile([P, T], U8, name="xs_all", align_bytes=64)
         nc.vector.memset(xs_all[:].bitcast(I32), 0)
-        xs_rows = keep.tile([P, T // 4], I32, name="xs_rows")
-        for q in range(4):
-            rows = slice(32 * q, 32 * q + 4 * PASSES)
-            nc.sync.dma_start(xs_rows[rows, :], x_scales[:, 4 * q : 4 * q + 4, :].bitcast(I32))
-            nc.vector.tensor_copy(xs_all[rows, :].bitcast(I32), xs_rows[rows, :])
+        xs_landed = keep.tile([P, T // 4], I32, name="xs_landed")
+        for q in range(QUADRANTS):
+            rows = slice(QUADRANT * q, QUADRANT * q + SCALE_ROWS * PASSES)
+            nc.sync.dma_start(
+                xs_landed[rows, :], x_scales[:, SCALE_ROWS * q : SCALE_ROWS * (q + 1), :].bitcast(I32)
+            )
+            nc.vector.tensor_copy(xs_all[rows, :].bitcast(I32), xs_landed[rows, :])
 
         xw_all = [keep.tile([P, T], I32, name=f"xw_all{g}", align_bytes=64) for g in range(PASSES)]
 
-        def load_x(g):
-            nc.sync.dma_start(xw_all[g][:], x_words[g].rearrange("p n t -> p (n t)").bitcast(I32))
-
-        def load_w(w, name, g, c0, c1):
+        def load_weights(w, name, g, c0, c1):
             raw = keep.tile([P, PACK, c1 - c0], F32, name=f"{name}_raw{g}_{c0}")
-            rows = w[g * K_PASS : (g + 1) * K_PASS, c0:c1]
-            nc.sync.dma_start(raw[:], rows.rearrange("(p j) c -> p j c", j=PACK))
+            k_rows = w[g * K_PASS : (g + 1) * K_PASS, c0:c1]
+            nc.sync.dma_start(raw[:], k_rows.rearrange("(p j) c -> p j c", j=PACK))
             return raw
 
-        w1_raw0 = load_w(w1, "w1", 0, 0, H)
-        load_x(0)
-        load_x(1)
-        w1_raw1 = load_w(w1, "w1", 1, 0, H)
+        w1_raw0 = load_weights(w1, "w1", 0, 0, H)
+        for g in range(PASSES):
+            nc.sync.dma_start(xw_all[g][:], x_words[g].rearrange("p n j -> p (n j)").bitcast(I32))
+        w1_raw1 = load_weights(w1, "w1", 1, 0, H)
         nc.sync.dma_start(src_sb[:], src)
-        w2_raw = [load_w(w2, "w2", g, 0, H) for g in range(PASSES)]
+        w2_raw0_first = load_weights(w2, "w2", 0, 0, W2_FIRST_ON_VECTOR)
+        w2_raw0_rest = load_weights(w2, "w2", 0, W2_FIRST_ON_VECTOR, H)
+        w2_raw1 = load_weights(w2, "w2", 1, 0, H)
         nc.sync.dma_start(dst_sb[:], dst)
         w3_codes = keep.tile([P, N], I32, name="w3_codes", align_bytes=64)
-        nc.sync.dma_start(w3_codes[:], w3_words[0].rearrange("p n t -> p (n t)").bitcast(I32))
-        w3_sc = keep.tile([P, N], U8, name="w3_sc", align_bytes=64)
-        nc.vector.memset(w3_sc[:].bitcast(I32), 0)
-        for q in range(4):
+        nc.sync.dma_start(w3_codes[:], w3_words[0].rearrange("p n j -> p (n j)").bitcast(I32))
+        w3_plane = keep.tile([P, N], U8, name="w3_plane", align_bytes=64)
+        nc.vector.memset(w3_plane[:].bitcast(I32), 0)
+        for q in range(QUADRANTS):
             nc.sync.dma_start(
-                w3_sc[32 * q : 32 * q + 4, :].bitcast(I32), w3_scales[0, 4 * q : 4 * q + 4, :].bitcast(I32)
+                w3_plane[QUADRANT * q : QUADRANT * q + SCALE_ROWS, :].bitcast(I32),
+                w3_scales[0, SCALE_ROWS * q : SCALE_ROWS * (q + 1), :].bitcast(I32),
             )
 
         xw = [keep.tile([P, S], U32, name=f"xw{g}", align_bytes=64) for g in range(PASSES)]
@@ -86,12 +98,18 @@ def tile_picked_hub_relu_p_kernel(
             scales = keep.tile([P, H], U8, name=f"{name}_scales{g}", align_bytes=64)
             return dealt, codes, scales
 
-        def deal_views(dealt, raw, c0, c1, walk="m j t"):
-            m0, m1 = c0 // PACK, c1 // PACK
+        def deal_views(tiles, raw_columns, c0):
+            m0, m1 = c0 // PACK, (c0 + raw_columns.shape[2]) // PACK
             return (
-                dealt[:, :, m0:m1, :].rearrange(f"p t m j -> p {walk}"),
-                raw[:, :, c0:c1].rearrange(f"p j (m t) -> p {walk}", t=PACK),
+                tiles[0][:, :, m0:m1, :].rearrange("p t m j -> p m j t"),
+                raw_columns.rearrange("p j (m t) -> p m j t", t=PACK),
             )
+
+        def deal_on_scalar(tiles, raw_columns, c0):
+            nc.scalar.activation(*deal_views(tiles, raw_columns, c0), ACT.Copy)
+
+        def deal_on_vector(tiles, raw_columns, c0):
+            nc.vector.tensor_copy(*deal_views(tiles, raw_columns, c0))
 
         def quantise_weights(tiles, t0, t1):
             dealt, codes, scales = tiles
@@ -101,130 +119,131 @@ def tile_picked_hub_relu_p_kernel(
                 in_=dealt[:, t0:t1, :, :].rearrange("p t m j -> p (t m j)"),
             )
 
-        def product(w_tiles, name, t, second_engine):
-            res = keep.tile([P, S], F32, name=f"{name}{t}")
-            width = BANK // 2 if second_engine else BANK
+        def product(w_passes, res, t, shared):
+            width = BANK // 2 if shared else BANK
             for h in range(S // width):
                 cols = slice(h * width, (h + 1) * width)
-                acc = acc_pool.tile([P, width], F32, name="acc", tag="acc")
+                acc = psum.tile([P, width], F32, name="acc", tag="bank")
                 for g in range(PASSES):
+                    codes, scales = w_passes[g][1:]
                     nc.tensor.matmul_mx(
                         out=acc[:],
-                        lhsT=w_tiles[g][1][:, t * P : (t + 1) * P].bitcast(FP8X4),
-                        lhsT_scale=w_tiles[g][2][:, t * P : (t + 1) * P],
+                        lhsT=codes[:, t * P : (t + 1) * P].bitcast(FP8X4),
+                        lhsT_scale=scales[:, t * P : (t + 1) * P],
                         rhs=xw[g][:, cols].bitcast(FP8X4),
-                        rhs_scale=xs[4 * g :, cols],
+                        rhs_scale=xs[SCALE_ROWS * g :, cols],
                         start=(g == 0),
                         stop=(g == PASSES - 1),
                     )
-                if h % 2 == 1 and second_engine:
+                if shared and h % 2 == 1:
                     nc.vector.tensor_copy(res[:, cols], acc[:])
                 else:
                     nc.scalar.copy(res[:, cols], acc[:])
-            return res
 
-        w1_q = [weight_tiles("w1", g) for g in range(PASSES)]
-        w2_q = [weight_tiles("w2", g) for g in range(PASSES)]
-        nc.scalar.activation(*deal_views(w1_q[0][0], w1_raw0, 0, H // 2), ACT.Copy)
-        nc.vector.tensor_copy(*deal_views(w1_q[0][0], w1_raw0, H // 2, H))
-        quantise_weights(w1_q[0], 0, PACK)
-        nc.vector.tensor_copy(xw[0][:], xw_all[0][:].bitcast(U32).indirect(offs_sb[:]))
-        nc.vector.tensor_copy(xw[1][:], xw_all[1][:].bitcast(U32).indirect(offs_sb[:]))
-        nc.scalar.activation(*deal_views(w1_q[1][0], w1_raw1, 0, 192), ACT.Copy)
-        nc.vector.tensor_copy(*deal_views(w1_q[1][0], w1_raw1, 192, H))
+        w1_passes = [weight_tiles("w1", g) for g in range(PASSES)]
+        w2_passes = [weight_tiles("w2", g) for g in range(PASSES)]
+        deal_on_scalar(w1_passes[0], w1_raw0[:, :, : H // 2], 0)
+        deal_on_vector(w1_passes[0], w1_raw0[:, :, H // 2 :], H // 2)
+        quantise_weights(w1_passes[0], 0, PACK)
+        for g in range(PASSES):
+            nc.vector.tensor_copy(xw[g][:], xw_all[g][:].bitcast(U32).indirect(offs_sb[:]))
+        deal_on_scalar(w1_passes[1], w1_raw1[:, :, :W1_LAST_ON_SCALAR], 0)
+        deal_on_vector(w1_passes[1], w1_raw1[:, :, W1_LAST_ON_SCALAR:], W1_LAST_ON_SCALAR)
         for t in range(PACK):
-            quantise_weights(w1_q[1], t, t + 1)
+            quantise_weights(w1_passes[1], t, t + 1)
 
-        def fetch_sources(y_t, t):
-            got = []
-            for h in range(HALVES):
-                half = keep.tile([P, BANK], F32, name=f"ysrc{t}_{h}", tag=f"ysrc{t}_{h}", align_bytes=64)
+        hold_tile = PACK - 2
+
+        def sources(t):
+            y_t = keep.tile([P, Y_WINDOW], F32, name=f"y{t}")
+            product(w1_passes, y_t, t, shared=(t == 0))
+            if t != hold_tile:
+                whole = keep.tile([P, S], F32, name=f"y_src{t}")
+                nc.vector.tensor_copy(whole[:], y_t[:].indirect(src_sb[:]))
+                return [whole[:, :BANK], whole[:, BANK:]]
+            halves = []
+            for h in range(S // BANK):
+                half = keep.tile([P, BANK], F32, name=f"y_src{t}_{h}", tag=f"y_src{t}_{h}", align_bytes=64)
                 nc.vector.tensor_copy(half[:], y_t[:].indirect(entries(src_sb, h * BANK, BANK)))
-                got.append(half)
-            return got
+                halves.append(half[:])
+            return halves
 
-        def deal_w2(piece, engine):
-            g, c = divmod(piece, 2)
-            dealt, raw = deal_views(w2_q[g][0], w2_raw[g], c * H // 2, (c + 1) * H // 2)
-            if engine == "s":
-                nc.scalar.activation(dealt, raw, ACT.Copy)
-            elif engine == "v":
-                nc.vector.tensor_copy(dealt, raw)
-            else:
-                nc.gpsimd.tensor_scalar(dealt, raw, 1.0, 0.0, ALU.mult, ALU.add)
+        deal_on_vector(w2_passes[0], w2_raw0_first[:], 0)
+        y_src = [sources(0), sources(1)]
+        deal_on_scalar(w2_passes[0], w2_raw0_rest[:], W2_FIRST_ON_VECTOR)
+        quantise_weights(w2_passes[0], 0, PACK)
+        y_src.append(sources(2))
+        for c0 in (0, H // 2):
+            deal_on_scalar(w2_passes[1], w2_raw1[:, :, c0 : c0 + H // 2], c0)
+        for t in range(PACK):
+            quantise_weights(w2_passes[1], t, t + 1)
+        y_src.append(sources(3))
 
-        y_src = []
-        y_src.append(fetch_sources(product(w1_q, "y", 0, True), 0))
-        y_src.append(fetch_sources(product(w1_q, "y", 1, False), 1))
-        deal_w2(0, "s")
-        deal_w2(1, "s")
-        quantise_weights(w2_q[0], 0, PACK)
-        y_src.append(fetch_sources(product(w1_q, "y", 2, False), 2))
-        deal_w2(2, "s")
-        deal_w2(3, "s")
-        for u in range(PACK):
-            quantise_weights(w2_q[1], u, u + 1)
-        y_src.append(fetch_sources(product(w1_q, "y", 3, False), 3))
-
-        e = [product(w2_q, "e", t, False) for t in range(PACK)]
+        e = []
+        for t in range(PACK):
+            e.append(keep.tile([P, S], F32, name=f"e{t}"))
+            product(w2_passes, e[t], t, shared=False)
 
         out_rows = out.rearrange("(h p) r -> p h r", p=P)
+        row_tiles = N // P
 
-        def finish(z_bf, r0, n, last):
+        def finish(z_bf, r0, last):
+            n = z_bf.shape[1]
             z_codes = keep.tile([P, n], U32, name=f"z_codes{r0}", align_bytes=64)
             z_scales = keep.tile([P, n], U8, name=f"z_scales{r0}", align_bytes=64)
             nc.vector.quantize_mx(
                 out=z_codes[:].bitcast(FP8X4), scales=z_scales[:], in_=z_bf[:].rearrange("p r t -> p (r t)")
             )
-            staged = keep.tile([P, N // P, n], F32, name=f"staged{r0}")
-            per_bank = 1 if last else N // P
-            for b in range(0, N // P, per_bank):
-                bank = acc_pool.tile([P, per_bank, n], F32, name="bank", tag="acc")
-                for k in range(per_bank):
-                    m_cols = slice((b + k) * P, (b + k + 1) * P)
+            staged = keep.tile([P, row_tiles, n], F32, name=f"staged{r0}")
+            per_bank = 1 if last else row_tiles
+            for h0 in range(0, row_tiles, per_bank):
+                res = psum.tile([P, per_bank, n], F32, name="res", tag="bank")
+                for h in range(per_bank):
+                    m_cols = slice((h0 + h) * P, (h0 + h + 1) * P)
                     nc.tensor.matmul_mx(
-                        out=bank[:, k, :],
+                        out=res[:, h, :],
                         lhsT=w3_codes[:, m_cols].bitcast(FP8X4),
-                        lhsT_scale=w3_sc[:, m_cols],
+                        lhsT_scale=w3_plane[:, m_cols],
                         rhs=z_codes[:].bitcast(FP8X4),
                         rhs_scale=z_scales[:],
                         start=True,
                         stop=True,
                     )
-                if b == 1:
-                    nc.vector.tensor_copy(staged[:, b : b + per_bank, :], bank[:])
+                if h0 > 0:
+                    nc.vector.tensor_copy(staged[:, h0 : h0 + per_bank, :], res[:])
                 else:
-                    nc.scalar.copy(staged[:, b : b + per_bank, :], bank[:])
+                    nc.scalar.copy(staged[:, h0 : h0 + per_bank, :], res[:])
             nc.sync.dma_start(out_rows[:, :, r0 : r0 + n], staged[:])
 
+        sum_tags = ("sums0", f"y_src{hold_tile}_0", f"z_bf{sum(EDGE_CHUNKS[0][:-1])}")
         r0 = 0
-        pending = []
+        unfinished = []
         for c, pieces in enumerate(EDGE_CHUNKS):
             n = sum(pieces)
             last = c + 1 == len(EDGE_CHUNKS)
-            pre = keep.tile([P, PACK, n], F32, name=f"pre{c}", tag=("pre0", "ysrc2_0", "z_bf256")[c], align_bytes=64)
+            sums = keep.tile([P, PACK, n], F32, name=f"sums{c}", tag=sum_tags[c], align_bytes=64)
             for t in range(PACK):
                 nc.vector.tensor_tensor(
-                    pre[:, t, :],
+                    sums[:, t, :],
                     e[t][:].indirect(entries(dst_sb, r0, n)),
                     y_src[t][r0 // BANK][:, r0 % BANK : r0 % BANK + n],
                     ALU.add,
                 )
-            made = []
+            rounded = []
             first = 0
             for width in pieces:
                 z_bf = keep.tile([P, width, PACK], BF16, name=f"z_bf{r0}", tag=f"z_bf{r0}", align_bytes=64)
-                woven = z_bf[:].rearrange("p (a i) t -> p a t i", i=4)
-                planes = pre[:, :, first : first + width].rearrange("p t (a i) -> p a t i", i=4)
+                woven = z_bf[:].rearrange("p (a i) t -> p a t i", i=LINE)
+                planes = sums[:, :, first : first + width].rearrange("p t (a i) -> p a t i", i=LINE)
                 if last:
                     nc.vector.tensor_scalar_max(woven, planes, 0.0)
                 else:
                     nc.scalar.activation(woven, planes, ACT.Relu)
-                made.append((z_bf, r0, width, last))
+                rounded.append((z_bf, r0, last))
                 first = first + width
                 r0 = r0 + width
-            for job in pending:
-                finish(*job)
-            pending = made
-        for job in pending:
-            finish(*job)
+            for piece in unfinished:
+                finish(*piece)
+            unfinished = rounded
+        for piece in unfinished:
+            finish(*piece)

@@ -28,7 +28,8 @@ LINE = 4
 
 Y_WINDOW = 1408
 
-W1_LAST_ON_SCALAR = 192
+W1_LAST_ON_SCALAR = 48
+PAIR = 2
 
 W2_FIRST_ON_VECTOR = 192
 
@@ -69,14 +70,12 @@ def tile_picked_hub_relu_p_kernel(
             nc.sync.dma_start(raw[:], k_rows.rearrange("(p j) c -> p j c", j=PACK))
             return raw
 
-        w1_raw0 = load_weights(w1, "w1", 0, 0, H)
+        w1_raw = []
         for g in range(PASSES):
             nc.sync.dma_start(xw_all[g][:], x_words[g].rearrange("p n j -> p (n j)").bitcast(I32))
-        w1_raw1 = load_weights(w1, "w1", 1, 0, H)
+            w1_raw.append(load_weights(w1, "w1", g, 0, H))
         nc.sync.dma_start(src_sb[:], src)
-        w2_raw0_first = load_weights(w2, "w2", 0, 0, W2_FIRST_ON_VECTOR)
-        w2_raw0_rest = load_weights(w2, "w2", 0, W2_FIRST_ON_VECTOR, H)
-        w2_raw1 = load_weights(w2, "w2", 1, 0, H)
+        w2_raw = [load_weights(w2, "w2", g, 0, H) for g in range(PASSES)]
         nc.sync.dma_start(dst_sb[:], dst)
         w3_codes = keep.tile([P, N], I32, name="w3_codes", align_bytes=64)
         nc.sync.dma_start(w3_codes[:], w3_words[0].rearrange("p n j -> p (n j)").bitcast(I32))
@@ -88,36 +87,32 @@ def tile_picked_hub_relu_p_kernel(
                 w3_scales[0, SCALE_ROWS * q : SCALE_ROWS * (q + 1), :].bitcast(I32),
             )
 
-        xw = [keep.tile([P, S], U32, name=f"xw{g}", align_bytes=64) for g in range(PASSES)]
+        xw = [keep.tile([P, S], U32, name="xw0", align_bytes=64)]
         xs = keep.tile([P, S], U8, name="xs", align_bytes=64)
-        nc.vector.tensor_copy(xs[:], xs_all[:].indirect(offs_sb[:]))
 
-        def weight_tiles(name, g):
-            dealt = keep.tile([P, PACK, P, PACK], BF16, name=f"{name}_bf{g}", align_bytes=64)
-            codes = keep.tile([P, H], U32, name=f"{name}_codes{g}", align_bytes=64)
-            scales = keep.tile([P, H], U8, name=f"{name}_scales{g}", align_bytes=64)
-            return dealt, codes, scales
+        def pair_tile(name):
+            return keep.tile([P, PAIR, P, PACK], BF16, name=f"{name}_bf", tag=f"{name}_bf", align_bytes=64)
 
-        def deal_views(tiles, raw_columns, c0):
-            m0, m1 = c0 // PACK, (c0 + raw_columns.shape[2]) // PACK
+        def deal_views(dealt, raw, pair, m0, m1):
             return (
-                tiles[0][:, :, m0:m1, :].rearrange("p t m j -> p m j t"),
-                raw_columns.rearrange("p j (m t) -> p m j t", t=PACK),
+                dealt[:, :, m0:m1, :].rearrange("p t m j -> p m j t"),
+                raw[:].rearrange("p j (m t) -> p m j t", t=PACK)[:, m0:m1, :, PAIR * pair : PAIR * (pair + 1)],
             )
 
-        def deal_on_scalar(tiles, raw_columns, c0):
-            nc.scalar.activation(*deal_views(tiles, raw_columns, c0), ACT.Copy)
+        def deal_on_scalar(dealt, raw, pair, m0=0, m1=P):
+            nc.scalar.activation(*deal_views(dealt, raw, pair, m0, m1), ACT.Copy)
 
-        def deal_on_vector(tiles, raw_columns, c0):
-            nc.vector.tensor_copy(*deal_views(tiles, raw_columns, c0))
+        def deal_on_vector(dealt, raw, pair, m0=0, m1=P):
+            nc.vector.tensor_copy(*deal_views(dealt, raw, pair, m0, m1))
 
-        def quantise_weights(tiles, t0, t1):
-            dealt, codes, scales = tiles
+        def quantise_weights(dealt, name, tag=None):
+            tiles = dealt.shape[1]
+            codes = keep.tile([P, tiles * P], U32, name=f"{name}_codes", tag=tag or f"{name}_codes", align_bytes=64)
+            scales = keep.tile([P, tiles * P], U8, name=f"{name}_scales", align_bytes=64)
             nc.vector.quantize_mx(
-                out=codes[:, t0 * P : t1 * P].bitcast(FP8X4),
-                scales=scales[:, t0 * P : t1 * P],
-                in_=dealt[:, t0:t1, :, :].rearrange("p t m j -> p (t m j)"),
+                out=codes[:].bitcast(FP8X4), scales=scales[:], in_=dealt.rearrange("p t m j -> p (t m j)")
             )
+            return [(codes[:, t * P : (t + 1) * P], scales[:, t * P : (t + 1) * P]) for t in range(tiles)]
 
         def product(w_passes, res, t, shared):
             width = BANK // 2 if shared else BANK
@@ -125,32 +120,34 @@ def tile_picked_hub_relu_p_kernel(
                 cols = slice(h * width, (h + 1) * width)
                 acc = psum.tile([P, width], F32, name="acc", tag="bank")
                 for g in range(PASSES):
-                    codes, scales = w_passes[g][1:]
+                    codes, scales = w_passes[g][t]
                     nc.tensor.matmul_mx(
                         out=acc[:],
-                        lhsT=codes[:, t * P : (t + 1) * P].bitcast(FP8X4),
-                        lhsT_scale=scales[:, t * P : (t + 1) * P],
+                        lhsT=codes.bitcast(FP8X4),
+                        lhsT_scale=scales,
                         rhs=xw[g][:, cols].bitcast(FP8X4),
                         rhs_scale=xs[SCALE_ROWS * g :, cols],
                         start=(g == 0),
                         stop=(g == PASSES - 1),
                     )
-                if shared and h % 2 == 1:
+                if shared and h % 2 == 0:
                     nc.vector.tensor_copy(res[:, cols], acc[:])
                 else:
                     nc.scalar.copy(res[:, cols], acc[:])
 
-        w1_passes = [weight_tiles("w1", g) for g in range(PASSES)]
-        w2_passes = [weight_tiles("w2", g) for g in range(PASSES)]
-        deal_on_scalar(w1_passes[0], w1_raw0[:, :, : H // 2], 0)
-        deal_on_vector(w1_passes[0], w1_raw0[:, :, H // 2 :], H // 2)
-        quantise_weights(w1_passes[0], 0, PACK)
-        for g in range(PASSES):
-            nc.vector.tensor_copy(xw[g][:], xw_all[g][:].bitcast(U32).indirect(offs_sb[:]))
-        deal_on_scalar(w1_passes[1], w1_raw1[:, :, :W1_LAST_ON_SCALAR], 0)
-        deal_on_vector(w1_passes[1], w1_raw1[:, :, W1_LAST_ON_SCALAR:], W1_LAST_ON_SCALAR)
-        for t in range(PACK):
-            quantise_weights(w1_passes[1], t, t + 1)
+        nc.vector.tensor_copy(xs[:], xs_all[:].indirect(offs_sb[:]))
+        nc.vector.tensor_copy(xw[0][:], xw_all[0][:].bitcast(U32).indirect(offs_sb[:]))
+        w1_00, w1_01, w1_10, w1_11 = [pair_tile(f"w1_{g}{pair}") for g in range(PASSES) for pair in range(2)]
+        deal_on_scalar(w1_00, w1_raw[0], 0)
+        deal_on_vector(w1_01, w1_raw[0], 1)
+        w1_passes = [quantise_weights(w1_00[:], "w1_00")]
+        xw.append(keep.tile([P, S], U32, name="xw1", tag="w1_00_bf", align_bytes=64))
+        nc.vector.tensor_copy(xw[1][:], xw_all[1][:].bitcast(U32).indirect(offs_sb[:]))
+        deal_on_scalar(w1_10, w1_raw[1], 0, 0, W1_LAST_ON_SCALAR)
+        deal_on_vector(w1_10, w1_raw[1], 0, W1_LAST_ON_SCALAR, P)
+        w1_passes.append(quantise_weights(w1_10[:, 0:1], "w1_10a") + quantise_weights(w1_10[:, 1:2], "w1_10b"))
+        w1_passes[0].extend(quantise_weights(w1_01[:], "w1_01", tag="w1_10_bf"))
+        deal_on_scalar(w1_11, w1_raw[1], 1, 0, P // 2)
 
         hold_tile = PACK - 2
 
@@ -168,16 +165,21 @@ def tile_picked_hub_relu_p_kernel(
                 halves.append(half[:])
             return halves
 
-        deal_on_vector(w2_passes[0], w2_raw0_first[:], 0)
-        y_src = [sources(0), sources(1)]
-        deal_on_scalar(w2_passes[0], w2_raw0_rest[:], W2_FIRST_ON_VECTOR)
-        quantise_weights(w2_passes[0], 0, PACK)
+        w2_00, w2_01, w2_10, w2_11 = [pair_tile(f"w2_{g}{pair}") for g in range(PASSES) for pair in range(2)]
+        y_src = [sources(0)]
+        deal_on_scalar(w1_11, w1_raw[1], 1, P // 2, P)
+        w1_passes[1].extend(quantise_weights(w1_11[:], "w1_11"))
+        y_src.append(sources(1))
+        deal_on_scalar(w2_00, w2_raw[0], 0)
+        w2_passes = [quantise_weights(w2_00[:], "w2_00")]
         y_src.append(sources(2))
-        for c0 in (0, H // 2):
-            deal_on_scalar(w2_passes[1], w2_raw1[:, :, c0 : c0 + H // 2], c0)
-        for t in range(PACK):
-            quantise_weights(w2_passes[1], t, t + 1)
+        deal_on_scalar(w2_10, w2_raw[1], 0)
+        w2_passes.append(quantise_weights(w2_10[:], "w2_10"))
+        deal_on_scalar(w2_01, w2_raw[0], 1)
+        w2_passes[0].extend(quantise_weights(w2_01[:], "w2_01"))
         y_src.append(sources(3))
+        deal_on_scalar(w2_11, w2_raw[1], 1)
+        w2_passes[1].extend(quantise_weights(w2_11[:], "w2_11"))
 
         e = []
         for t in range(PACK):

@@ -30,6 +30,7 @@ Y_WINDOW = 1408
 
 W1_LAST_ON_SCALAR = 48
 PAIR = 2
+PLACE_BYTES = 9216
 
 W2_FIRST_ON_VECTOR = 192
 
@@ -42,55 +43,65 @@ def tile_picked_hub_relu_p_kernel(
     nc = tc.nc
     with ExitStack() as ctx:
         keep = ctx.enter_context(tc.tile_pool(name="keep", bufs=1))
-        psum = ctx.enter_context(tc.psum_pool(name="psum", bufs=8))
+        reused = ctx.enter_context(tc.tile_pool(name="reused", bufs=1))
+        psum = ctx.enter_context(tc.psum_pool(name="psum", bufs=1))
 
         def entries(list_tile, first, count):
             return list_tile[:, first // STRIPE : (first + count) // STRIPE]
+
+        places = {}
+
+        def place(shape, dtype, name, on=None, shift=0):
+            if on is None:
+                return keep.tile(shape, dtype, name=name, align_bytes=64)
+            offset = places.setdefault(on, 64 + PLACE_BYTES * len(places)) + shift
+            return reused.tile(shape, dtype, name=name, align_bytes=64, offset=offset)
 
         offs_sb = keep.tile([P, S // STRIPE], U16, name="offs_sb")
         src_sb = keep.tile([P, S // STRIPE], U16, name="src_sb")
         dst_sb = keep.tile([P, S // STRIPE], U16, name="dst_sb")
         nc.sync.dma_start(offs_sb[:], offs)
 
+        rows_at = P - QUADRANT
         xs_all = keep.tile([P, T], U8, name="xs_all", align_bytes=64)
-        nc.vector.memset(xs_all[:].bitcast(I32), 0)
-        xs_landed = keep.tile([P, T // 4], I32, name="xs_landed")
-        for q in range(QUADRANTS):
-            rows = slice(QUADRANT * q, QUADRANT * q + SCALE_ROWS * PASSES)
-            nc.sync.dma_start(
-                xs_landed[rows, :], x_scales[:, SCALE_ROWS * q : SCALE_ROWS * (q + 1), :].bitcast(I32)
-            )
-            nc.vector.tensor_copy(xs_all[rows, :].bitcast(I32), xs_landed[rows, :])
+        nc.vector.memset(xs_all[:rows_at, :].bitcast(I32), 0)
+        nc.sync.dma_start(xs_all[rows_at:, :].bitcast(I32), x_scales.rearrange("g r n -> (g r) n").bitcast(I32))
 
-        xw_all = [keep.tile([P, T], I32, name=f"xw_all{g}", align_bytes=64) for g in range(PASSES)]
+        xw_all = [place([P, T], I32, f"xw_all{g}", f"xw_all{g}") for g in range(PASSES)]
 
-        def load_weights(w, name, g, c0, c1):
-            raw = keep.tile([P, PACK, c1 - c0], F32, name=f"{name}_raw{g}_{c0}")
-            k_rows = w[g * K_PASS : (g + 1) * K_PASS, c0:c1]
+        def load_words(g):
+            nc.sync.dma_start(xw_all[g][:], x_words[g].rearrange("p n j -> p (n j)").bitcast(I32))
+
+        def load_weights(w, name, g, on, shift=0):
+            raw = place([P, PACK, H], F32, f"{name}_raw{g}", on, shift)
+            k_rows = w[g * K_PASS : (g + 1) * K_PASS, :]
             nc.sync.dma_start(raw[:], k_rows.rearrange("(p j) c -> p j c", j=PACK))
             return raw
 
-        w1_raw = []
-        for g in range(PASSES):
-            nc.sync.dma_start(xw_all[g][:], x_words[g].rearrange("p n j -> p (n j)").bitcast(I32))
-            w1_raw.append(load_weights(w1, "w1", g, 0, H))
+        load_words(0)
+        w1_raw = [load_weights(w1, "w1", 0, "w1_raw0")]
+        load_words(1)
         nc.sync.dma_start(src_sb[:], src)
-        w2_raw = [load_weights(w2, "w2", g, 0, H) for g in range(PASSES)]
         nc.sync.dma_start(dst_sb[:], dst)
-        w3_codes = keep.tile([P, N], I32, name="w3_codes", align_bytes=64)
-        nc.sync.dma_start(w3_codes[:], w3_words[0].rearrange("p n j -> p (n j)").bitcast(I32))
-        w3_plane = keep.tile([P, N], U8, name="w3_plane", align_bytes=64)
-        nc.vector.memset(w3_plane[:].bitcast(I32), 0)
-        for q in range(QUADRANTS):
-            nc.sync.dma_start(
-                w3_plane[QUADRANT * q : QUADRANT * q + SCALE_ROWS, :].bitcast(I32),
-                w3_scales[0, SCALE_ROWS * q : SCALE_ROWS * (q + 1), :].bitcast(I32),
-            )
 
         xw = [keep.tile([P, S], U32, name="xw0", align_bytes=64)]
-        xs = keep.tile([P, S], U8, name="xs", align_bytes=64)
+        xs_picked = keep.tile([P, S], U8, name="xs_picked", align_bytes=64)
+        xs = []
+
+        def scale_plane(g, on, shift):
+            plane = place([P, S], U8, f"xs{g}", on, shift)
+            nc.vector.memset(plane[:].bitcast(I32), 0)
+            for q in range(QUADRANTS):
+                row = rows_at + SCALE_ROWS * (QUADRANTS * g + q)
+                nc.sync.dma_start(
+                    plane[QUADRANT * q : QUADRANT * q + SCALE_ROWS, :].bitcast(I32),
+                    xs_picked[row : row + SCALE_ROWS, :].bitcast(I32),
+                )
+            xs.append(plane)
 
         def pair_tile(name):
+            if name in ("w1_00", "w1_01"):
+                return place([P, PAIR, P, PACK], BF16, f"{name}_bf", "tile1_codes", 4096 + 2048 * int(name[-1]))
             return keep.tile([P, PAIR, P, PACK], BF16, name=f"{name}_bf", tag=f"{name}_bf", align_bytes=64)
 
         def deal_views(dealt, raw, pair, m0, m1):
@@ -107,18 +118,21 @@ def tile_picked_hub_relu_p_kernel(
 
         def quantise_weights(dealt, name, tag=None):
             tiles = dealt.shape[1]
-            codes = keep.tile([P, tiles * P], U32, name=f"{name}_codes", tag=tag or f"{name}_codes", align_bytes=64)
+            if name in ("w1_10a", "w1_11"):
+                codes = place([P, tiles * P], U32, f"{name}_codes", "tile1_codes")
+            else:
+                codes = keep.tile([P, tiles * P], U32, name=f"{name}_codes", tag=tag or f"{name}_codes", align_bytes=64)
             scales = keep.tile([P, tiles * P], U8, name=f"{name}_scales", align_bytes=64)
             nc.vector.quantize_mx(
                 out=codes[:].bitcast(FP8X4), scales=scales[:], in_=dealt.rearrange("p t m j -> p (t m j)")
             )
             return [(codes[:, t * P : (t + 1) * P], scales[:, t * P : (t + 1) * P]) for t in range(tiles)]
 
-        def product(w_passes, res, t, shared):
+        def product(w_passes, res, t, shared, bank, only=None):
             width = BANK // 2 if shared else BANK
-            for h in range(S // width):
+            for h in range(S // width) if only is None else [only]:
                 cols = slice(h * width, (h + 1) * width)
-                acc = psum.tile([P, width], F32, name="acc", tag="bank")
+                acc = psum.tile([P, width], F32, name="acc", tag=f"bank{bank + h}")
                 for g in range(PASSES):
                     codes, scales = w_passes[g][t]
                     nc.tensor.matmul_mx(
@@ -126,7 +140,7 @@ def tile_picked_hub_relu_p_kernel(
                         lhsT=codes.bitcast(FP8X4),
                         lhsT_scale=scales,
                         rhs=xw[g][:, cols].bitcast(FP8X4),
-                        rhs_scale=xs[SCALE_ROWS * g :, cols],
+                        rhs_scale=xs[g][:, cols],
                         start=(g == 0),
                         stop=(g == PASSES - 1),
                     )
@@ -135,35 +149,44 @@ def tile_picked_hub_relu_p_kernel(
                 else:
                     nc.scalar.copy(res[:, cols], acc[:])
 
-        nc.vector.tensor_copy(xs[:], xs_all[:].indirect(offs_sb[:]))
+        nc.vector.tensor_copy(xs_picked[:], xs_all[:].indirect(offs_sb[:]))
+        scale_plane(0, None, 0)
         nc.vector.tensor_copy(xw[0][:], xw_all[0][:].bitcast(U32).indirect(offs_sb[:]))
+        w1_raw.append(load_weights(w1, "w1", 1, "xw_all0", -64))
+        scale_plane(1, "xw_all0", 8192 - 64)
         w1_00, w1_01, w1_10, w1_11 = [pair_tile(f"w1_{g}{pair}") for g in range(PASSES) for pair in range(2)]
         deal_on_scalar(w1_00, w1_raw[0], 0)
         deal_on_vector(w1_01, w1_raw[0], 1)
-        w1_passes = [quantise_weights(w1_00[:], "w1_00")]
-        xw.append(keep.tile([P, S], U32, name="xw1", tag="w1_00_bf", align_bytes=64))
+        w1_passes = [quantise_weights(w1_00[:], "w1_00") + quantise_weights(w1_01[:], "w1_01")]
+        w2_raw = [load_weights(w2, "w2", 0, "w1_raw0", -64)]
+        xw.append(place([P, S], U32, "xw1", "tile1_codes", 4096))
         nc.vector.tensor_copy(xw[1][:], xw_all[1][:].bitcast(U32).indirect(offs_sb[:]))
+        w2_raw.append(load_weights(w2, "w2", 1, "xw_all1", -64))
+        w3_codes = place([P, N], I32, "w3_codes", "xw_all1", 8192 - 64)
+        nc.sync.dma_start(w3_codes[:], w3_words[0].rearrange("p n j -> p (n j)").bitcast(I32))
+        w3_plane = place([P, N], U8, "w3_plane", "w1_raw0", 8192 - 64)
+        nc.gpsimd.memset(w3_plane[:].bitcast(I32), 0)
+        for q in range(QUADRANTS):
+            nc.sync.dma_start(
+                w3_plane[QUADRANT * q : QUADRANT * q + SCALE_ROWS, :].bitcast(I32),
+                w3_scales[0, SCALE_ROWS * q : SCALE_ROWS * (q + 1), :].bitcast(I32),
+            )
         deal_on_scalar(w1_10, w1_raw[1], 0, 0, W1_LAST_ON_SCALAR)
         deal_on_vector(w1_10, w1_raw[1], 0, W1_LAST_ON_SCALAR, P)
         w1_passes.append(quantise_weights(w1_10[:, 0:1], "w1_10a") + quantise_weights(w1_10[:, 1:2], "w1_10b"))
-        w1_passes[0].extend(quantise_weights(w1_01[:], "w1_01", tag="w1_10_bf"))
         deal_on_scalar(w1_11, w1_raw[1], 1, 0, P // 2)
 
-        hold_tile = PACK - 2
+        wide, narrow = 256, 128
+        late = wide + narrow
+        area = keep.tile([P, late + PACK * wide], F32, name="area", align_bytes=64)
+        z_area = keep.tile([P, 3 * BANK], F32, name="z_area", align_bytes=64)
 
         def sources(t):
             y_t = keep.tile([P, Y_WINDOW], F32, name=f"y{t}")
-            product(w1_passes, y_t, t, shared=(t == 0))
-            if t != hold_tile:
-                whole = keep.tile([P, S], F32, name=f"y_src{t}")
-                nc.vector.tensor_copy(whole[:], y_t[:].indirect(src_sb[:]))
-                return [whole[:, :BANK], whole[:, BANK:]]
-            halves = []
-            for h in range(S // BANK):
-                half = keep.tile([P, BANK], F32, name=f"y_src{t}_{h}", tag=f"y_src{t}_{h}", align_bytes=64)
-                nc.vector.tensor_copy(half[:], y_t[:].indirect(entries(src_sb, h * BANK, BANK)))
-                halves.append(half[:])
-            return halves
+            product(w1_passes, y_t, t, t == 0, (0, 4, 0, 2)[t])
+            whole = area[:, :S] if t == 2 else keep.tile([P, S], F32, name=f"y_src{t}")[:]
+            nc.vector.tensor_copy(whole, y_t[:].indirect(src_sb[:]))
+            return whole
 
         w2_00, w2_01, w2_10, w2_11 = [pair_tile(f"w2_{g}{pair}") for g in range(PASSES) for pair in range(2)]
         y_src = [sources(0)]
@@ -181,25 +204,31 @@ def tile_picked_hub_relu_p_kernel(
         deal_on_scalar(w2_11, w2_raw[1], 1)
         w2_passes[1].extend(quantise_weights(w2_11[:], "w2_11"))
 
-        e = []
-        for t in range(PACK):
-            e.append(keep.tile([P, S], F32, name=f"e{t}"))
-            product(w2_passes, e[t], t, shared=False)
+        e = [keep.tile([P, S], F32, name=f"e{t}") for t in range(PACK)]
+        for t, h in ((0, 0), (0, 1), (1, 0), (1, 1), (3, 0), (2, 0), (2, 1), (3, 1)):
+            product(w2_passes, e[t], t, False, (6, 4, 0, 2)[t], only=h)
 
         out_rows = out.rearrange("(h p) r -> p h r", p=P)
         row_tiles = N // P
 
-        def finish(z_bf, r0, last):
+        banks_used = []
+
+        def finish(z_bf, r0, last, parts=1):
             n = z_bf.shape[1]
             z_codes = keep.tile([P, n], U32, name=f"z_codes{r0}", align_bytes=64)
             z_scales = keep.tile([P, n], U8, name=f"z_scales{r0}", align_bytes=64)
-            nc.vector.quantize_mx(
-                out=z_codes[:].bitcast(FP8X4), scales=z_scales[:], in_=z_bf[:].rearrange("p r t -> p (r t)")
-            )
+            for c0 in range(0, n, n // parts):
+                cols = slice(c0, c0 + n // parts)
+                nc.vector.quantize_mx(
+                    out=z_codes[:, cols].bitcast(FP8X4),
+                    scales=z_scales[:, cols],
+                    in_=z_bf[:, cols, :].rearrange("p r t -> p (r t)"),
+                )
             staged = keep.tile([P, row_tiles, n], F32, name=f"staged{r0}")
             per_bank = 1 if last else row_tiles
             for h0 in range(0, row_tiles, per_bank):
-                res = psum.tile([P, per_bank, n], F32, name="res", tag="bank")
+                res = psum.tile([P, per_bank, n], F32, name="res", tag=f"bank{(6, 7, 4, 5, 0, 1)[len(banks_used)]}")
+                banks_used.append(r0)
                 for h in range(per_bank):
                     m_cols = slice((h0 + h) * P, (h0 + h + 1) * P)
                     nc.tensor.matmul_mx(
@@ -217,35 +246,52 @@ def tile_picked_hub_relu_p_kernel(
                     nc.scalar.copy(staged[:, h0 : h0 + per_bank, :], res[:])
             nc.sync.dma_start(out_rows[:, :, r0 : r0 + n], staged[:])
 
-        sum_tags = ("sums0", f"y_src{hold_tile}_0", f"z_bf{sum(EDGE_CHUNKS[0][:-1])}")
-        r0 = 0
-        unfinished = []
-        for c, pieces in enumerate(EDGE_CHUNKS):
-            n = sum(pieces)
-            last = c + 1 == len(EDGE_CHUNKS)
-            sums = keep.tile([P, PACK, n], F32, name=f"sums{c}", tag=sum_tags[c], align_bytes=64)
-            for t in range(PACK):
-                nc.vector.tensor_tensor(
-                    sums[:, t, :],
-                    e[t][:].indirect(entries(dst_sb, r0, n)),
-                    y_src[t][r0 // BANK][:, r0 % BANK : r0 % BANK + n],
-                    ALU.add,
-                )
-            rounded = []
-            first = 0
-            for width in pieces:
-                z_bf = keep.tile([P, width, PACK], BF16, name=f"z_bf{r0}", tag=f"z_bf{r0}", align_bytes=64)
-                woven = z_bf[:].rearrange("p (a i) t -> p a t i", i=LINE)
-                planes = sums[:, :, first : first + width].rearrange("p t (a i) -> p a t i", i=LINE)
-                if last:
-                    nc.vector.tensor_scalar_max(woven, planes, 0.0)
-                else:
-                    nc.scalar.activation(woven, planes, ACT.Relu)
-                rounded.append((z_bf, r0, last))
-                first = first + width
-                r0 = r0 + width
-            for piece in unfinished:
-                finish(*piece)
-            unfinished = rounded
-        for piece in unfinished:
-            finish(*piece)
+        def add(sums, t, r0):
+            n = sums.shape[2]
+            nc.vector.tensor_tensor(
+                sums[:, t, :],
+                e[t][:].indirect(entries(dst_sb, r0, n)),
+                y_src[t][:, r0 : r0 + n],
+                ALU.add,
+            )
+
+        def planes_in(area, at, n):
+            return area[:, at : at + PACK * n].rearrange("p (t r) -> p t r", t=PACK)
+
+        def z_in(area, at, n):
+            return area[:, at : at + PAIR * n].bitcast(BF16).rearrange("p (r t) -> p r t", t=PACK)
+
+        def relu(z_bf, sums, on_vector=False):
+            woven = z_bf.rearrange("p (a i) t -> p a t i", i=LINE)
+            planes = sums.rearrange("p t (a i) -> p a t i", i=LINE)
+            if on_vector:
+                nc.vector.tensor_scalar_max(woven, planes, 0.0)
+            else:
+                nc.scalar.activation(woven, planes, ACT.Relu)
+
+        def z_tile(name, n):
+            return keep.tile([P, n, PACK], BF16, name=name, align_bytes=64)[:]
+
+        sums0 = keep.tile([P, PACK, S - late], F32, name="sums0")[:]
+        for t in range(PACK):
+            add(sums0, t, late)
+        z0 = z_in(z_area, 0, BANK)
+        z0_last = z_in(area, 0, narrow)
+        relu(z0, sums0[:, :, :BANK])
+        sums1 = planes_in(area, late, wide)
+        for t in range(PACK):
+            add(sums1, t, narrow)
+        z1 = z_in(z_area, 2 * BANK, wide)
+        relu(z1, sums1)
+        finish(z0[:, wide:, :], late + wide, False)
+        finish(z0[:, :wide, :], late, False)
+        sums2 = planes_in(z_area, 2 * BANK - (PACK - 1) * narrow, narrow)
+        for t in range(PACK - 1):
+            add(sums2, t, 0)
+        finish(z1, narrow, False, parts=2)
+        add(sums2, PACK - 1, 0)
+        relu(z0_last, sums0[:, :, BANK:], on_vector=True)
+        z2 = z_tile("z2", narrow)
+        relu(z2, sums2, on_vector=True)
+        finish(z0_last, late + BANK, False)
+        finish(z2, 0, True)

@@ -213,7 +213,7 @@ def tile_picked_hub_relu_p_kernel(
 
         banks_used = []
 
-        def finish(z_bf, r0, last, parts=1):
+        def finish(z_bf, r0, last, parts=1, split=False):
             n = z_bf.shape[1]
             z_codes = keep.tile([P, n], U32, name=f"z_codes{r0}", align_bytes=64)
             z_scales = keep.tile([P, n], U8, name=f"z_scales{r0}", align_bytes=64)
@@ -225,9 +225,9 @@ def tile_picked_hub_relu_p_kernel(
                     in_=z_bf[:, cols, :].rearrange("p r t -> p (r t)"),
                 )
             staged = keep.tile([P, row_tiles, n], F32, name=f"staged{r0}")
-            per_bank = 1 if last else row_tiles
+            per_bank = 1 if last or split else row_tiles
             for h0 in range(0, row_tiles, per_bank):
-                res = psum.tile([P, per_bank, n], F32, name="res", tag=f"bank{(6, 7, 4, 5, 0, 1)[len(banks_used)]}")
+                res = psum.tile([P, per_bank, n], F32, name="res", tag=f"bank{(6, 7, 4, 5, 0, 1, 2, 3)[len(banks_used)]}")
                 banks_used.append(r0)
                 for h in range(per_bank):
                     m_cols = slice((h0 + h) * P, (h0 + h + 1) * P)
@@ -240,11 +240,15 @@ def tile_picked_hub_relu_p_kernel(
                         start=True,
                         stop=True,
                     )
-                if h0 > 0:
+                if h0 > 0 and last:
                     nc.vector.tensor_copy(staged[:, h0 : h0 + per_bank, :], res[:])
                 else:
                     nc.scalar.copy(staged[:, h0 : h0 + per_bank, :], res[:])
-            nc.sync.dma_start(out_rows[:, :, r0 : r0 + n], staged[:])
+            if last or split:
+                (nc.scalar if last else nc.sync).dma_start(out_rows[:, 0, r0 : r0 + n], staged[:, 0, :])
+                nc.sync.dma_start(out_rows[:, 1, r0 : r0 + n], staged[:, 1, :])
+            else:
+                nc.sync.dma_start(out_rows[:, :, r0 : r0 + n], staged[:])
 
         def add(sums, t, r0):
             n = sums.shape[2]
@@ -288,10 +292,10 @@ def tile_picked_hub_relu_p_kernel(
         sums2 = planes_in(z_area, 2 * BANK - (PACK - 1) * narrow, narrow)
         for t in range(PACK - 1):
             add(sums2, t, 0)
-        finish(z1, narrow, False, parts=2)
+        finish(z1, narrow, False, parts=2, split=True)
         add(sums2, PACK - 1, 0)
         relu(z0_last, sums0[:, :, BANK:], on_vector=True)
         z2 = z_tile("z2", narrow)
         relu(z2, sums2, on_vector=True)
-        finish(z0_last, late + BANK, False)
+        finish(z0_last, late + BANK, True)
         finish(z2, 0, True)

@@ -277,8 +277,10 @@ def tile_picked_hub_relu_p_kernel(
             return keep.tile([P, n, PACK], BF16, name=name, align_bytes=64)[:]
 
         sums0 = keep.tile([P, PACK, S - late], F32, name="sums0")[:]
-        for t in range(PACK):
+        for t in range(PACK - 1):
             add(sums0, t, late)
+        add(sums0[:, :, :BANK], PACK - 1, late)
+        add(sums0[:, :, BANK:], PACK - 1, late + BANK)
         z0 = z_in(z_area, 0, BANK)
         z0_last = z_in(area, 0, narrow)
         relu(z0, sums0[:, :, :BANK])

@@ -194,12 +194,11 @@ def tile_picked_hub_relu_p_kernel(
         w1_passes[1].extend(quantise_weights(w1_11[:], "w1_11"))
         y_src.append(sources(1))
         deal_on_scalar(w2_00, w2_raw[0], 0)
-        w2_passes = [quantise_weights(w2_00[:], "w2_00")]
+        deal_on_scalar(w2_01, w2_raw[0], 1)
+        w2_passes = [quantise_weights(w2_00[:], "w2_00") + quantise_weights(w2_01[:], "w2_01")]
         y_src.append(sources(2))
         deal_on_scalar(w2_10, w2_raw[1], 0)
         w2_passes.append(quantise_weights(w2_10[:], "w2_10"))
-        deal_on_scalar(w2_01, w2_raw[0], 1)
-        w2_passes[0].extend(quantise_weights(w2_01[:], "w2_01"))
         y_src.append(sources(3))
         deal_on_scalar(w2_11, w2_raw[1], 1)
         w2_passes[1].extend(quantise_weights(w2_11[:], "w2_11"))
@@ -231,15 +230,17 @@ def tile_picked_hub_relu_p_kernel(
                 banks_used.append(r0)
                 for h in range(per_bank):
                     m_cols = slice((h0 + h) * P, (h0 + h + 1) * P)
-                    nc.tensor.matmul_mx(
-                        out=res[:, h, :],
-                        lhsT=w3_codes[:, m_cols].bitcast(FP8X4),
-                        lhsT_scale=w3_plane[:, m_cols],
-                        rhs=z_codes[:].bitcast(FP8X4),
-                        rhs_scale=z_scales[:],
-                        start=True,
-                        stop=True,
-                    )
+                    for c0 in range(0, n, n // parts):
+                        cols = slice(c0, c0 + n // parts)
+                        nc.tensor.matmul_mx(
+                            out=res[:, h, cols],
+                            lhsT=w3_codes[:, m_cols].bitcast(FP8X4),
+                            lhsT_scale=w3_plane[:, m_cols],
+                            rhs=z_codes[:, cols].bitcast(FP8X4),
+                            rhs_scale=z_scales[:, cols],
+                            start=True,
+                            stop=True,
+                        )
                 if h0 > 0 and last:
                     nc.vector.tensor_copy(staged[:, h0 : h0 + per_bank, :], res[:])
                 else:

@@ -26,15 +26,14 @@ BANK = 512
 STRIPE = 16
 LINE = 4
 
-Y_WINDOW = 1408
+WINDOW = S + STRIPE
 
 W1_LAST_ON_SCALAR = 48
 PAIR = 2
 PLACE_BYTES = 9216
 
-W2_FIRST_ON_VECTOR = 192
-
-EDGE_CHUNKS = ((256, 256), (256, 128), (128,))
+HALF = S // 2
+QUARTER = S // 4
 
 
 def tile_picked_hub_relu_p_kernel(
@@ -84,7 +83,7 @@ def tile_picked_hub_relu_p_kernel(
         nc.sync.dma_start(src_sb[:], src)
         nc.sync.dma_start(dst_sb[:], dst)
 
-        xw = [keep.tile([P, S], U32, name="xw0", align_bytes=64)]
+        xw = [place([P, S], U32, "xw0", "xw0")]
         xs_picked = keep.tile([P, S], U8, name="xs_picked", align_bytes=64)
         xs = []
 
@@ -128,12 +127,13 @@ def tile_picked_hub_relu_p_kernel(
             )
             return [(codes[:, t * P : (t + 1) * P], scales[:, t * P : (t + 1) * P]) for t in range(tiles)]
 
-        def product(w_passes, res, t, shared, bank, only=None):
-            width = BANK // 2 if shared else BANK
-            for h in range(S // width) if only is None else [only]:
+        def product(w_passes, name, t, first_bank, emptiers, order=(0, 1)):
+            res = keep.tile([P, WINDOW], F32, name=f"{name}{t}")
+            width = S // len(emptiers)
+            for h, empty in enumerate(emptiers):
                 cols = slice(h * width, (h + 1) * width)
-                acc = psum.tile([P, width], F32, name="acc", tag=f"bank{bank + h}")
-                for g in range(PASSES):
+                acc = psum.tile([P, width], F32, name="acc", tag=f"bank{first_bank + h}")
+                for g in order:
                     codes, scales = w_passes[g][t]
                     nc.tensor.matmul_mx(
                         out=acc[:],
@@ -141,13 +141,13 @@ def tile_picked_hub_relu_p_kernel(
                         lhsT_scale=scales,
                         rhs=xw[g][:, cols].bitcast(FP8X4),
                         rhs_scale=xs[g][:, cols],
-                        start=(g == 0),
-                        stop=(g == PASSES - 1),
+                        start=(g == order[0]),
+                        stop=(g == order[-1]),
                     )
-                if shared and h % 2 == 0:
-                    nc.vector.tensor_copy(res[:, cols], acc[:])
-                else:
-                    nc.scalar.copy(res[:, cols], acc[:])
+                empty(res[:, cols], acc[:])
+            return res
+
+        on_vector, on_scalar = nc.vector.tensor_copy, nc.scalar.copy
 
         nc.vector.tensor_copy(xs_picked[:], xs_all[:].indirect(offs_sb[:]))
         scale_plane(0, None, 0)
@@ -176,129 +176,106 @@ def tile_picked_hub_relu_p_kernel(
         w1_passes.append(quantise_weights(w1_10[:, 0:1], "w1_10a") + quantise_weights(w1_10[:, 1:2], "w1_10b"))
         deal_on_scalar(w1_11, w1_raw[1], 1, 0, P // 2)
 
-        wide, narrow = 256, 128
-        late = wide + narrow
-        area = keep.tile([P, late + PACK * wide], F32, name="area", align_bytes=64)
-        z_area = keep.tile([P, 3 * BANK], F32, name="z_area", align_bytes=64)
+        deal_on_vector(w1_11, w1_raw[1], 1, P // 2, P)
 
-        def sources(t):
-            y_t = keep.tile([P, Y_WINDOW], F32, name=f"y{t}")
-            product(w1_passes, y_t, t, t == 0, (0, 4, 0, 2)[t])
-            whole = area[:, :S] if t == 2 else keep.tile([P, S], F32, name=f"y_src{t}")[:]
-            nc.vector.tensor_copy(whole, y_t[:].indirect(src_sb[:]))
-            return whole
-
-        w2_00, w2_01, w2_10, w2_11 = [pair_tile(f"w2_{g}{pair}") for g in range(PASSES) for pair in range(2)]
-        y_src = [sources(0)]
-        deal_on_scalar(w1_11, w1_raw[1], 1, P // 2, P)
-        w1_passes[1].extend(quantise_weights(w1_11[:], "w1_11"))
-        y_src.append(sources(1))
-        deal_on_scalar(w2_00, w2_raw[0], 0)
-        deal_on_scalar(w2_01, w2_raw[0], 1)
-        w2_passes = [quantise_weights(w2_00[:], "w2_00") + quantise_weights(w2_01[:], "w2_01")]
-        y_src.append(sources(2))
-        deal_on_scalar(w2_10, w2_raw[1], 0)
-        w2_passes.append(quantise_weights(w2_10[:], "w2_10"))
-        y_src.append(sources(3))
-        deal_on_scalar(w2_11, w2_raw[1], 1)
-        w2_passes[1].extend(quantise_weights(w2_11[:], "w2_11"))
-
-        e = [keep.tile([P, S], F32, name=f"e{t}") for t in range(PACK)]
-        for t, h in ((0, 0), (0, 1), (1, 0), (1, 1), (3, 0), (2, 0), (2, 1), (3, 1)):
-            product(w2_passes, e[t], t, False, (6, 4, 0, 2)[t], only=h)
-
+        area = keep.tile([P, PACK * S], F32, name="area")
+        sums = area[:].rearrange("p (t r) -> p t r", t=PACK)
+        last = S - QUARTER
         out_rows = out.rearrange("(h p) r -> p h r", p=P)
         row_tiles = N // P
 
-        banks_used = []
+        def fetch(got, y_t, r0):
+            nc.scalar.activation(got, y_t[:].indirect(entries(src_sb, r0, got.shape[1])), ACT.Copy)
+            return got
 
-        def finish(z_bf, r0, last, parts=1, split=False):
-            n = z_bf.shape[1]
-            z_codes = keep.tile([P, n], U32, name=f"z_codes{r0}", align_bytes=64)
-            z_scales = keep.tile([P, n], U8, name=f"z_scales{r0}", align_bytes=64)
-            for c0 in range(0, n, n // parts):
-                cols = slice(c0, c0 + n // parts)
-                nc.vector.quantize_mx(
-                    out=z_codes[:, cols].bitcast(FP8X4),
-                    scales=z_scales[:, cols],
-                    in_=z_bf[:, cols, :].rearrange("p r t -> p (r t)"),
-                )
-            staged = keep.tile([P, row_tiles, n], F32, name=f"staged{r0}")
-            per_bank = 1 if last or split else row_tiles
-            for h0 in range(0, row_tiles, per_bank):
-                res = psum.tile([P, per_bank, n], F32, name="res", tag=f"bank{(6, 7, 4, 5, 0, 1, 2, 3)[len(banks_used)]}")
-                banks_used.append(r0)
-                for h in range(per_bank):
-                    m_cols = slice((h0 + h) * P, (h0 + h + 1) * P)
-                    for c0 in range(0, n, n // parts):
-                        cols = slice(c0, c0 + n // parts)
-                        nc.tensor.matmul_mx(
-                            out=res[:, h, cols],
-                            lhsT=w3_codes[:, m_cols].bitcast(FP8X4),
-                            lhsT_scale=w3_plane[:, m_cols],
-                            rhs=z_codes[:, cols].bitcast(FP8X4),
-                            rhs_scale=z_scales[:, cols],
-                            start=True,
-                            stop=True,
-                        )
-                if h0 > 0 and last:
-                    nc.vector.tensor_copy(staged[:, h0 : h0 + per_bank, :], res[:])
-                else:
-                    nc.scalar.copy(staged[:, h0 : h0 + per_bank, :], res[:])
-            if last or split:
-                (nc.scalar if last else nc.sync).dma_start(out_rows[:, 0, r0 : r0 + n], staged[:, 0, :])
-                nc.sync.dma_start(out_rows[:, 1, r0 : r0 + n], staged[:, 1, :])
-            else:
-                nc.sync.dma_start(out_rows[:, :, r0 : r0 + n], staged[:])
+        def add(plane, e_t, r0, got):
+            nc.vector.tensor_tensor(plane, e_t[:].indirect(entries(dst_sb, r0, plane.shape[1])), got, ALU.add)
 
-        def add(sums, t, r0):
-            n = sums.shape[2]
-            nc.vector.tensor_tensor(
-                sums[:, t, :],
-                e[t][:].indirect(entries(dst_sb, r0, n)),
-                y_src[t][:, r0 : r0 + n],
-                ALU.add,
-            )
-
-        def planes_in(area, at, n):
-            return area[:, at : at + PACK * n].rearrange("p (t r) -> p t r", t=PACK)
-
-        def z_in(area, at, n):
-            return area[:, at : at + PAIR * n].bitcast(BF16).rearrange("p (r t) -> p r t", t=PACK)
-
-        def relu(z_bf, sums, on_vector=False):
-            woven = z_bf.rearrange("p (a i) t -> p a t i", i=LINE)
-            planes = sums.rearrange("p t (a i) -> p a t i", i=LINE)
-            if on_vector:
+        def relu(planes, name, vector):
+            z_bf = keep.tile([P, planes.shape[2], PACK], BF16, name=name, align_bytes=64)
+            woven = z_bf[:].rearrange("p (a i) t -> p a t i", i=LINE)
+            planes = planes.rearrange("p t (a i) -> p a t i", i=LINE)
+            if vector:
                 nc.vector.tensor_scalar_max(woven, planes, 0.0)
             else:
                 nc.scalar.activation(woven, planes, ACT.Relu)
+            return z_bf
 
-        def z_tile(name, n):
-            return keep.tile([P, n, PACK], BF16, name=name, align_bytes=64)[:]
+        def quantise_z(z_bf, r0):
+            n = z_bf.shape[1]
+            z_codes = keep.tile([P, n], U32, name=f"z_codes{r0}", align_bytes=64)
+            z_scales = keep.tile([P, n], U8, name=f"z_scales{r0}", align_bytes=64)
+            nc.vector.quantize_mx(
+                out=z_codes[:].bitcast(FP8X4), scales=z_scales[:], in_=z_bf[:].rearrange("p r t -> p (r t)")
+            )
+            return z_codes, z_scales
 
-        sums0 = keep.tile([P, PACK, S - late], F32, name="sums0")[:]
-        for t in range(PACK - 1):
-            add(sums0, t, late)
-        add(sums0[:, :, :BANK], PACK - 1, late)
-        add(sums0[:, :, BANK:], PACK - 1, late + BANK)
-        z0 = z_in(z_area, 0, BANK)
-        z0_last = z_in(area, 0, narrow)
-        relu(z0, sums0[:, :, :BANK])
-        sums1 = planes_in(area, late, wide)
-        for t in range(PACK):
-            add(sums1, t, narrow)
-        z1 = z_in(z_area, 2 * BANK, wide)
-        relu(z1, sums1)
-        finish(z0[:, wide:, :], late + wide, False)
-        finish(z0[:, :wide, :], late, False)
-        sums2 = planes_in(z_area, 2 * BANK - (PACK - 1) * narrow, narrow)
-        for t in range(PACK - 1):
-            add(sums2, t, 0)
-        finish(z1, narrow, False, parts=2, split=True)
-        add(sums2, PACK - 1, 0)
-        relu(z0_last, sums0[:, :, BANK:], on_vector=True)
-        z2 = z_tile("z2", narrow)
-        relu(z2, sums2, on_vector=True)
-        finish(z0_last, late + BANK, True)
-        finish(z2, 0, True)
+        def finish(z_mx, r0, banks, emptiers, queues):
+            z_codes, z_scales = z_mx
+            n = z_codes.shape[1]
+            per_bank = row_tiles // len(banks)
+            staged = keep.tile([P, row_tiles, n], F32, name=f"staged{r0}")
+            for b, bank in enumerate(banks):
+                rows = slice(b * per_bank, (b + 1) * per_bank)
+                res = psum.tile([P, per_bank, n], F32, name="res", tag=f"bank{bank}")
+                for h in range(per_bank):
+                    m_cols = slice((b * per_bank + h) * P, (b * per_bank + h + 1) * P)
+                    nc.tensor.matmul_mx(
+                        out=res[:, h, :],
+                        lhsT=w3_codes[:, m_cols].bitcast(FP8X4),
+                        lhsT_scale=w3_plane[:, m_cols],
+                        rhs=z_codes[:].bitcast(FP8X4),
+                        rhs_scale=z_scales[:],
+                        start=True,
+                        stop=True,
+                    )
+                emptiers[b](staged[:, rows, :], res[:])
+                queues[b].dma_start(out_rows[:, rows, r0 : r0 + n], staged[:, rows, :])
+
+        w2_00, w2_01, w2_10, w2_11 = [pair_tile(f"w2_{g}{pair}") for g in range(PASSES) for pair in range(2)]
+        y0 = product(w1_passes, "y", 0, 0, (on_vector, on_scalar, on_vector, on_scalar))
+        ys0 = fetch(keep.tile([P, S], F32, name="ys0")[:], y0, 0)
+        w1_passes[1].extend(quantise_weights(w1_11[:], "w1_11"))
+        deal_on_vector(w2_00, w2_raw[0], 0)
+        y1 = product(w1_passes, "y", 1, 4, (on_vector, on_scalar))
+        ys1 = fetch(place([P, S], F32, "ys1", "xw0", 4096)[:], y1, 0)
+        w2_passes = [quantise_weights(w2_00[:], "w2_00")]
+        deal_on_vector(w2_10, w2_raw[1], 0)
+        deal_on_vector(w2_01, w2_raw[0], 1)
+        w2_passes.append(quantise_weights(w2_10[:], "w2_10"))
+        y2 = product(w1_passes, "y", 2, 0, (on_scalar, on_scalar))
+        y3 = product(w1_passes, "y", 3, 2, (on_scalar, on_scalar))
+        deal_on_vector(w2_11, w2_raw[1], 1)
+        w2_passes[0].extend(quantise_weights(w2_01[:], "w2_01"))
+        e0 = product(w2_passes, "e", 0, 6, (on_vector, on_vector))
+        w2_passes[1].extend(quantise_weights(w2_11[:], "w2_11"))
+        ys2_early = fetch(sums[:, 2, HALF:], y2, 0)
+        ys3_early = fetch(sums[:, 3, HALF:], y3, 0)
+        e1 = product(w2_passes, "e", 1, 4, (on_vector, on_vector))
+        add(sums[:, 0, :], e0, 0, ys0)
+        e2 = product(w2_passes, "e", 2, 0, (on_scalar, on_scalar), (1, 0))
+        e3 = product(w2_passes, "e", 3, 2, (on_scalar, on_scalar), (1, 0))
+        add(sums[:, 1, :], e1, 0, ys1)
+        add(sums[:, 2, :HALF], e2, 0, ys2_early)
+        add(sums[:, 3, :HALF], e3, 0, ys3_early)
+        ys_late = place([P, S], F32, "ys_late", "xw0", 2048)
+        ys2_late = fetch(ys_late[:, :HALF], y2, HALF)
+        ys3_late = fetch(ys_late[:, HALF:], y3, HALF)
+        add(sums[:, 2, HALF:last], e2, HALF, ys2_late[:, :QUARTER])
+        z_a = relu(sums[:, :, :QUARTER], "z_a", True)
+        z_b = relu(sums[:, :, QUARTER:HALF], "z_b", False)
+        add(sums[:, 3, HALF:last], e3, HALF, ys3_late[:, :QUARTER])
+        mx_a = quantise_z(z_a, 0)
+        z_c = relu(sums[:, :, HALF:last], "z_c", False)
+        add(sums[:, 2, last:], e2, last, ys2_late[:, QUARTER:])
+        mx_b = quantise_z(z_b, QUARTER)
+        add(sums[:, 3, last:], e3, last, ys3_late[:, QUARTER:])
+        finish(mx_a, 0, (6,), (on_scalar,), (nc.sync,))
+        finish(mx_b, QUARTER, (7,), (on_scalar,), (nc.sync,))
+        mx_c = quantise_z(z_c, HALF)
+        eighth = QUARTER // 2
+        z_d = relu(sums[:, :, last : last + eighth], "z_d", False)
+        z_e = relu(sums[:, :, last + eighth :], "z_e", True)
+        finish(mx_c, HALF, (4,), (on_scalar,), (nc.sync,))
+        finish(quantise_z(z_e, last + eighth), last + eighth, (5,), (on_vector,), (nc.sync,))
+        finish(quantise_z(z_d, last), last, (0, 1), (on_scalar, on_vector), (nc.scalar, nc.sync))

@@ -26,7 +26,7 @@ BANK = 512
 STRIPE = 16
 LINE = 4
 
-WINDOW = S + STRIPE
+WINDOW = 1408
 
 W1_LAST_ON_SCALAR = 48
 PAIR = 2
@@ -83,7 +83,7 @@ def tile_picked_hub_relu_p_kernel(
         nc.sync.dma_start(src_sb[:], src)
         nc.sync.dma_start(dst_sb[:], dst)
 
-        xw = [place([P, S], U32, "xw0", "xw0")]
+        xw = [keep.tile([P, S], U32, name="xw0", align_bytes=64)]
         xs_picked = keep.tile([P, S], U8, name="xs_picked", align_bytes=64)
         xs = []
 
@@ -127,8 +127,8 @@ def tile_picked_hub_relu_p_kernel(
             )
             return [(codes[:, t * P : (t + 1) * P], scales[:, t * P : (t + 1) * P]) for t in range(tiles)]
 
-        def product(w_passes, name, t, first_bank, emptiers, order=(0, 1)):
-            res = keep.tile([P, WINDOW], F32, name=f"{name}{t}")
+        def product(w_passes, name, t, first_bank, emptiers, order=(0, 1), on=None):
+            res = place([P, WINDOW], F32, f"{name}{t}", on)
             width = S // len(emptiers)
             for h, empty in enumerate(emptiers):
                 cols = slice(h * width, (h + 1) * width)
@@ -232,50 +232,54 @@ def tile_picked_hub_relu_p_kernel(
                 emptiers[b](staged[:, rows, :], res[:])
                 queues[b].dma_start(out_rows[:, rows, r0 : r0 + n], staged[:, rows, :])
 
-        w2_00, w2_01, w2_10, w2_11 = [pair_tile(f"w2_{g}{pair}") for g in range(PASSES) for pair in range(2)]
+        w2_00, w2_01 = pair_tile("w2_00"), pair_tile("w2_01")
+        relay = keep.tile([P, S], F32, name="relay", align_bytes=64)
+        w2_10, w2_11 = [
+            half.bitcast(BF16).rearrange("p (t m j) -> p t m j", t=PAIR, j=PACK)
+            for half in (relay[:, :HALF], relay[:, HALF:])
+        ]
         y0 = product(w1_passes, "y", 0, 0, (on_vector, on_scalar, on_vector, on_scalar))
         ys0 = fetch(keep.tile([P, S], F32, name="ys0")[:], y0, 0)
         w1_passes[1].extend(quantise_weights(w1_11[:], "w1_11"))
         deal_on_vector(w2_00, w2_raw[0], 0)
-        y1 = product(w1_passes, "y", 1, 4, (on_vector, on_scalar))
-        ys1 = fetch(place([P, S], F32, "ys1", "xw0", 4096)[:], y1, 0)
+        y1 = product(w1_passes, "y", 1, 4, (on_scalar, on_scalar), on="y1")
+        deal_on_vector(w2_01, w2_raw[0], 1)
         w2_passes = [quantise_weights(w2_00[:], "w2_00")]
         deal_on_vector(w2_10, w2_raw[1], 0)
-        deal_on_vector(w2_01, w2_raw[0], 1)
-        w2_passes.append(quantise_weights(w2_10[:], "w2_10"))
+        w2_passes[0].extend(quantise_weights(w2_01[:], "w2_01"))
+        deal_on_vector(w2_11, w2_raw[1], 1)
+        w2_passes.append(quantise_weights(w2_10, "w2_10") + quantise_weights(w2_11, "w2_11"))
         y2 = product(w1_passes, "y", 2, 0, (on_scalar, on_scalar))
         y3 = product(w1_passes, "y", 3, 2, (on_scalar, on_scalar))
-        deal_on_vector(w2_11, w2_raw[1], 1)
-        w2_passes[0].extend(quantise_weights(w2_01[:], "w2_01"))
-        e0 = product(w2_passes, "e", 0, 6, (on_vector, on_vector))
-        w2_passes[1].extend(quantise_weights(w2_11[:], "w2_11"))
-        ys2_early = fetch(sums[:, 2, HALF:], y2, 0)
-        ys3_early = fetch(sums[:, 3, HALF:], y3, 0)
-        e1 = product(w2_passes, "e", 1, 4, (on_vector, on_vector))
+        e0 = product(w2_passes, "e", 0, 6, (on_vector, on_scalar))
+        ys1 = relay[:]
+        nc.vector.tensor_copy(ys1, y1[:].indirect(src_sb[:]))
+        e1 = product(w2_passes, "e", 1, 4, (on_scalar, on_scalar))
+        ys_early = place([P, S], F32, "ys_early", "y1")
+        ys2_early = fetch(ys_early[:, :HALF], y2, 0)
+        ys3_early = fetch(ys_early[:, HALF:], y3, 0)
         add(sums[:, 0, :], e0, 0, ys0)
         e2 = product(w2_passes, "e", 2, 0, (on_scalar, on_scalar), (1, 0))
         e3 = product(w2_passes, "e", 3, 2, (on_scalar, on_scalar), (1, 0))
         add(sums[:, 1, :], e1, 0, ys1)
         add(sums[:, 2, :HALF], e2, 0, ys2_early)
-        add(sums[:, 3, :HALF], e3, 0, ys3_early)
-        ys_late = place([P, S], F32, "ys_late", "xw0", 2048)
-        ys2_late = fetch(ys_late[:, :HALF], y2, HALF)
-        ys3_late = fetch(ys_late[:, HALF:], y3, HALF)
-        add(sums[:, 2, HALF:last], e2, HALF, ys2_late[:, :QUARTER])
+        add(sums[:, 3, :QUARTER], e3, 0, ys3_early[:, :QUARTER])
+        add(sums[:, 3, QUARTER:HALF], e3, QUARTER, ys3_early[:, QUARTER:])
+        ys2_late = fetch(relay[:, :HALF], y2, HALF)
+        ys3_late = fetch(relay[:, HALF:], y3, HALF)
         z_a = relu(sums[:, :, :QUARTER], "z_a", True)
         z_b = relu(sums[:, :, QUARTER:HALF], "z_b", False)
-        add(sums[:, 3, HALF:last], e3, HALF, ys3_late[:, :QUARTER])
-        mx_a = quantise_z(z_a, 0)
-        z_c = relu(sums[:, :, HALF:last], "z_c", False)
+        add(sums[:, 2, HALF:last], e2, HALF, ys2_late[:, :QUARTER])
+        finish(quantise_z(z_a, 0), 0, (6,), (on_scalar,), (nc.sync,))
         add(sums[:, 2, last:], e2, last, ys2_late[:, QUARTER:])
-        mx_b = quantise_z(z_b, QUARTER)
-        add(sums[:, 3, last:], e3, last, ys3_late[:, QUARTER:])
-        finish(mx_a, 0, (6,), (on_scalar,), (nc.sync,))
-        finish(mx_b, QUARTER, (7,), (on_scalar,), (nc.sync,))
-        mx_c = quantise_z(z_c, HALF)
+        add(sums[:, 3, HALF:last], e3, HALF, ys3_late[:, :QUARTER])
+        finish(quantise_z(z_b, QUARTER), QUARTER, (7,), (on_scalar,), (nc.sync,))
         eighth = QUARTER // 2
+        add(sums[:, 3, last : last + eighth], e3, last, ys3_late[:, QUARTER : QUARTER + eighth])
+        z_c = relu(sums[:, :, HALF:last], "z_c", True)
         z_d = relu(sums[:, :, last : last + eighth], "z_d", False)
+        add(sums[:, 3, last + eighth :], e3, last + eighth, ys3_late[:, QUARTER + eighth :])
+        finish(quantise_z(z_c, HALF), HALF, (4, 2), (on_scalar, on_scalar), (nc.sync, nc.sync))
         z_e = relu(sums[:, :, last + eighth :], "z_e", True)
-        finish(mx_c, HALF, (4,), (on_scalar,), (nc.sync,))
-        finish(quantise_z(z_e, last + eighth), last + eighth, (5,), (on_vector,), (nc.sync,))
-        finish(quantise_z(z_d, last), last, (0, 1), (on_scalar, on_vector), (nc.scalar, nc.sync))
+        finish(quantise_z(z_d, last), last, (5,), (on_vector,), (nc.sync,))
+        finish(quantise_z(z_e, last + eighth), last + eighth, (0, 1), (on_scalar, on_vector), (nc.scalar, nc.sync))

@@ -232,9 +232,9 @@ def tile_picked_hub_relu_p_kernel(
                 emptiers[b](staged[:, rows, :], res[:])
                 queues[b].dma_start(out_rows[:, rows, r0 : r0 + n], staged[:, rows, :])
 
-        w2_00, w2_01 = pair_tile("w2_00"), pair_tile("w2_01")
+        w2_01, w2_11 = pair_tile("w2_01"), pair_tile("w2_11")
         relay = keep.tile([P, S], F32, name="relay", align_bytes=64)
-        w2_10, w2_11 = [
+        w2_00, w2_10 = [
             half.bitcast(BF16).rearrange("p (t m j) -> p t m j", t=PAIR, j=PACK)
             for half in (relay[:, :HALF], relay[:, HALF:])
         ]
@@ -242,24 +242,24 @@ def tile_picked_hub_relu_p_kernel(
         ys0 = fetch(keep.tile([P, S], F32, name="ys0")[:], y0, 0)
         w1_passes[1].extend(quantise_weights(w1_11[:], "w1_11"))
         deal_on_vector(w2_00, w2_raw[0], 0)
-        y1 = product(w1_passes, "y", 1, 4, (on_scalar, on_scalar), on="y1")
+        y1 = product(w1_passes, "y", 1, 4, (on_vector, on_vector), on="y1")
         deal_on_vector(w2_01, w2_raw[0], 1)
-        w2_passes = [quantise_weights(w2_00[:], "w2_00")]
+        w2_passes = [quantise_weights(w2_00, "w2_00")]
         deal_on_vector(w2_10, w2_raw[1], 0)
         w2_passes[0].extend(quantise_weights(w2_01[:], "w2_01"))
         deal_on_vector(w2_11, w2_raw[1], 1)
-        w2_passes.append(quantise_weights(w2_10, "w2_10") + quantise_weights(w2_11, "w2_11"))
+        w2_passes.append(quantise_weights(w2_10, "w2_10") + quantise_weights(w2_11[:], "w2_11"))
         y2 = product(w1_passes, "y", 2, 0, (on_scalar, on_scalar))
         y3 = product(w1_passes, "y", 3, 2, (on_scalar, on_scalar))
-        e0 = product(w2_passes, "e", 0, 6, (on_vector, on_scalar))
+        e0 = product(w2_passes, "e", 0, 6, (on_scalar, on_scalar))
         ys1 = relay[:]
         nc.vector.tensor_copy(ys1, y1[:].indirect(src_sb[:]))
         e1 = product(w2_passes, "e", 1, 4, (on_scalar, on_scalar))
         ys_early = place([P, S], F32, "ys_early", "y1")
         ys2_early = fetch(ys_early[:, :HALF], y2, 0)
-        ys3_early = fetch(ys_early[:, HALF:], y3, 0)
         add(sums[:, 0, :], e0, 0, ys0)
         e2 = product(w2_passes, "e", 2, 0, (on_scalar, on_scalar), (1, 0))
+        ys3_early = fetch(ys_early[:, HALF:], y3, 0)
         e3 = product(w2_passes, "e", 3, 2, (on_scalar, on_scalar), (1, 0))
         add(sums[:, 1, :], e1, 0, ys1)
         add(sums[:, 2, :HALF], e2, 0, ys2_early)

@@ -40,6 +40,7 @@ def tile_picked_hub_relu_p_kernel(
     tc, x_words, x_scales, w1, w2, w3_words, w3_scales, offs, src, dst, out
 ):
     nc = tc.nc
+    w1, w2, src, dst = w2, w1, dst, src
     with ExitStack() as ctx:
         keep = ctx.enter_context(tc.tile_pool(name="keep", bufs=1))
         reused = ctx.enter_context(tc.tile_pool(name="reused", bufs=1))

@@ -163,21 +163,21 @@ def tile_picked_hub_relu_p_kernel(
         xw.append(place([P, S], U32, "xw1", "tile1_codes", 4096))
         nc.vector.tensor_copy(xw[1][:], xw_all[1][:].bitcast(U32).indirect(offs_sb[:]))
         w2_raw.append(load_weights(w2, "w2", 1, "xw_all1", -64))
-        w3_codes = place([P, N], I32, "w3_codes", "xw_all1", 8192 - 64)
-        nc.sync.dma_start(w3_codes[:], w3_words[0].rearrange("p n j -> p (n j)").bitcast(I32))
-        w3_plane = place([P, N], U8, "w3_plane", "w1_raw0", 8192 - 64)
-        nc.gpsimd.memset(w3_plane[:].bitcast(I32), 0)
-        for q in range(QUADRANTS):
-            nc.sync.dma_start(
-                w3_plane[QUADRANT * q : QUADRANT * q + SCALE_ROWS, :].bitcast(I32),
-                w3_scales[0, SCALE_ROWS * q : SCALE_ROWS * (q + 1), :].bitcast(I32),
-            )
         deal_on_scalar(w1_10, w1_raw[1], 0, 0, W1_LAST_ON_SCALAR)
         deal_on_vector(w1_10, w1_raw[1], 0, W1_LAST_ON_SCALAR, P)
         w1_passes.append(quantise_weights(w1_10[:, 0:1], "w1_10a") + quantise_weights(w1_10[:, 1:2], "w1_10b"))
         deal_on_scalar(w1_11, w1_raw[1], 1, 0, P // 2)
 
         deal_on_vector(w1_11, w1_raw[1], 1, P // 2, P)
+        w3_codes = place([P, N], I32, "w3_codes", "xw_all0")
+        nc.sync.dma_start(w3_codes[:], w3_words[0].rearrange("p n j -> p (n j)").bitcast(I32))
+        w3_plane = place([P, N], U8, "w3_plane", "xw_all0", 1024)
+        nc.gpsimd.memset(w3_plane[:].bitcast(I32), 0)
+        for q in range(QUADRANTS):
+            nc.sync.dma_start(
+                w3_plane[QUADRANT * q : QUADRANT * q + SCALE_ROWS, :].bitcast(I32),
+                w3_scales[0, SCALE_ROWS * q : SCALE_ROWS * (q + 1), :].bitcast(I32),
+            )
 
         area = keep.tile([P, PACK * S], F32, name="area")
         sums = area[:].rearrange("p (t r) -> p t r", t=PACK)
@@ -243,7 +243,7 @@ def tile_picked_hub_relu_p_kernel(
         ys0 = fetch(keep.tile([P, S], F32, name="ys0")[:], y0, 0)
         w1_passes[1].extend(quantise_weights(w1_11[:], "w1_11"))
         deal_on_vector(w2_00, w2_raw[0], 0)
-        y1 = product(w1_passes, "y", 1, 4, (on_vector, on_vector), on="y1")
+        y1 = product(w1_passes, "y", 1, 4, (on_vector, on_scalar), on="y1")
         deal_on_vector(w2_01, w2_raw[0], 1)
         w2_passes = [quantise_weights(w2_00, "w2_00")]
         deal_on_vector(w2_10, w2_raw[1], 0)

@@ -81,8 +81,6 @@ def tile_picked_hub_relu_p_kernel(
         load_words(0)
         w1_raw = [load_weights(w1, "w1", 0, "w1_raw0")]
         load_words(1)
-        nc.sync.dma_start(src_sb[:], src)
-        nc.sync.dma_start(dst_sb[:], dst)
 
         xw = [keep.tile([P, S], U32, name="xw0", align_bytes=64)]
         xs_picked = keep.tile([P, S], U8, name="xs_picked", align_bytes=64)
@@ -153,8 +151,9 @@ def tile_picked_hub_relu_p_kernel(
         nc.vector.tensor_copy(xs_picked[:], xs_all[:].indirect(offs_sb[:]))
         scale_plane(0, None, 0)
         nc.vector.tensor_copy(xw[0][:], xw_all[0][:].bitcast(U32).indirect(offs_sb[:]))
-        w1_raw.append(load_weights(w1, "w1", 1, "xw_all0", -64))
-        scale_plane(1, "xw_all0", 8192 - 64)
+        w1_raw.append(load_weights(w1, "w1", 1, "w1_raw1"))
+        scale_plane(1, None, 0)
+        nc.sync.dma_start(src_sb[:], src)
         w1_00, w1_01, w1_10, w1_11 = [pair_tile(f"w1_{g}{pair}") for g in range(PASSES) for pair in range(2)]
         deal_on_scalar(w1_00, w1_raw[0], 0)
         deal_on_vector(w1_01, w1_raw[0], 1)
@@ -162,16 +161,17 @@ def tile_picked_hub_relu_p_kernel(
         w2_raw = [load_weights(w2, "w2", 0, "w1_raw0", -64)]
         xw.append(place([P, S], U32, "xw1", "tile1_codes", 4096))
         nc.vector.tensor_copy(xw[1][:], xw_all[1][:].bitcast(U32).indirect(offs_sb[:]))
-        w2_raw.append(load_weights(w2, "w2", 1, "xw_all1", -64))
+        w2_raw.append(load_weights(w2, "w2", 1, None))
+        nc.sync.dma_start(dst_sb[:], dst)
         deal_on_scalar(w1_10, w1_raw[1], 0, 0, W1_LAST_ON_SCALAR)
         deal_on_vector(w1_10, w1_raw[1], 0, W1_LAST_ON_SCALAR, P)
         w1_passes.append(quantise_weights(w1_10[:, 0:1], "w1_10a") + quantise_weights(w1_10[:, 1:2], "w1_10b"))
         deal_on_scalar(w1_11, w1_raw[1], 1, 0, P // 2)
 
         deal_on_vector(w1_11, w1_raw[1], 1, P // 2, P)
-        w3_codes = place([P, N], I32, "w3_codes", "xw_all0")
+        w3_codes = place([P, N], I32, "w3_codes", "w1_raw1")
         nc.sync.dma_start(w3_codes[:], w3_words[0].rearrange("p n j -> p (n j)").bitcast(I32))
-        w3_plane = place([P, N], U8, "w3_plane", "xw_all0", 1024)
+        w3_plane = place([P, N], U8, "w3_plane", "w1_raw1", 1024)
         nc.gpsimd.memset(w3_plane[:].bitcast(I32), 0)
         for q in range(QUADRANTS):
             nc.sync.dma_start(

@@ -169,10 +169,10 @@ def tile_picked_hub_relu_p_kernel(
         deal_on_scalar(w1_11, w1_raw[1], 1, 0, P // 2)
 
         deal_on_vector(w1_11, w1_raw[1], 1, P // 2, P)
-        w3_codes = place([P, N], I32, "w3_codes", "w1_raw1")
+        w3_codes = place([P, N], I32, "w3_codes")
         nc.sync.dma_start(w3_codes[:], w3_words[0].rearrange("p n j -> p (n j)").bitcast(I32))
-        w3_plane = place([P, N], U8, "w3_plane", "w1_raw1", 1024)
-        nc.gpsimd.memset(w3_plane[:].bitcast(I32), 0)
+        w3_plane = place([P, N], U8, "w3_plane")
+        nc.vector.memset(w3_plane[:].bitcast(I32), 0)
         for q in range(QUADRANTS):
             nc.sync.dma_start(
                 w3_plane[QUADRANT * q : QUADRANT * q + SCALE_ROWS, :].bitcast(I32),

@@ -250,18 +250,18 @@ def tile_picked_hub_relu_p_kernel(
         w2_passes[0].extend(quantise_weights(w2_01[:], "w2_01"))
         deal_on_vector(w2_11, w2_raw[1], 1)
         w2_passes.append(quantise_weights(w2_10, "w2_10") + quantise_weights(w2_11[:], "w2_11"))
-        y2 = product(w1_passes, "y", 2, 0, (on_scalar, on_scalar))
-        y3 = product(w1_passes, "y", 3, 2, (on_scalar, on_scalar))
-        e0 = product(w2_passes, "e", 0, 6, (on_scalar, on_scalar))
+        y2 = product(w1_passes, "y", 2, 6, (on_scalar, on_scalar))
+        y3 = product(w1_passes, "y", 3, 0, (on_scalar, on_scalar))
+        e0 = product(w2_passes, "e", 0, 2, (on_scalar, on_scalar))
         ys1 = relay[:]
         nc.vector.tensor_copy(ys1, y1[:].indirect(src_sb[:]))
         e1 = product(w2_passes, "e", 1, 4, (on_scalar, on_scalar))
         ys_early = place([P, S], F32, "ys_early", "y1")
         ys2_early = fetch(ys_early[:, :HALF], y2, 0)
         add(sums[:, 0, :], e0, 0, ys0)
-        e2 = product(w2_passes, "e", 2, 0, (on_scalar, on_scalar), (1, 0))
+        e2 = product(w2_passes, "e", 2, 6, (on_scalar, on_scalar), (1, 0))
         ys3_early = fetch(ys_early[:, HALF:], y3, 0)
-        e3 = product(w2_passes, "e", 3, 2, (on_scalar, on_scalar), (1, 0))
+        e3 = product(w2_passes, "e", 3, 0, (on_scalar, on_scalar), (1, 0))
         add(sums[:, 1, :], e1, 0, ys1)
         add(sums[:, 2, :HALF], e2, 0, ys2_early)
         add(sums[:, 3, :QUARTER], e3, 0, ys3_early[:, :QUARTER])

from contextlib import ExitStack

import concourse.mybir as mybir

K, T, S, H, N = 1024, 2048, 1024, 512, 256
FLOPS = 2 * (2 * K * H * S + H * N * S)

F32 = mybir.dt.float32
BF16 = mybir.dt.bfloat16
I32 = mybir.dt.int32
U32 = mybir.dt.uint32
U16 = mybir.dt.uint16
U8 = mybir.dt.uint8
FP8X4 = mybir.dt.float8_e4m3fn_x4
ACT = mybir.ActivationFunctionType
ALU = mybir.AluOpType

P = 128
PACK = 4
K_PASS = P * PACK
PASSES = K // K_PASS
QUADRANTS = 4
QUADRANT = P // QUADRANTS
SCALE_ROWS = 4
BANK = 512
STRIPE = 16
LINE = 4

WINDOW = 1408

W1_LAST_ON_SCALAR = 48
PAIR = 2
PLACE_BYTES = 9216

HALF = S // 2
QUARTER = S // 4


def tile_picked_hub_relu_p_kernel(
    tc, x_words, x_scales, w1, w2, w3_words, w3_scales, offs, src, dst, out
):
    nc = tc.nc
    w1, w2, src, dst = w2, w1, dst, src
    with ExitStack() as ctx:
        keep = ctx.enter_context(tc.tile_pool(name="keep", bufs=1))
        reused = ctx.enter_context(tc.tile_pool(name="reused", bufs=1))
        psum = ctx.enter_context(tc.psum_pool(name="psum", bufs=1))

        def entries(list_tile, first, count):
            return list_tile[:, first // STRIPE : (first + count) // STRIPE]

        places = {}

        def place(shape, dtype, name, on=None, shift=0):
            if on is None:
                return keep.tile(shape, dtype, name=name, align_bytes=64)
            offset = places.setdefault(on, 64 + PLACE_BYTES * len(places)) + shift
            return reused.tile(shape, dtype, name=name, align_bytes=64, offset=offset)

        offs_sb = keep.tile([P, S // STRIPE], U16, name="offs_sb")
        src_sb = keep.tile([P, S // STRIPE], U16, name="src_sb")
        dst_sb = keep.tile([P, S // STRIPE], U16, name="dst_sb")
        nc.sync.dma_start(offs_sb[:], offs)

        rows_at = P - QUADRANT
        xs_all = keep.tile([P, T], U8, name="xs_all", align_bytes=64)
        nc.vector.memset(xs_all[:rows_at, :].bitcast(I32), 0)
        nc.sync.dma_start(xs_all[rows_at:, :].bitcast(I32), x_scales.rearrange("g r n -> (g r) n").bitcast(I32))

        xw_all = [place([P, T], I32, f"xw_all{g}", f"xw_all{g}") for g in range(PASSES)]

        def load_words(g):
            nc.sync.dma_start(xw_all[g][:], x_words[g].rearrange("p n j -> p (n j)").bitcast(I32))

        def load_weights(w, name, g, on, shift=0):
            raw = place([P, PACK, H], F32, f"{name}_raw{g}", on, shift)
            k_rows = w[g * K_PASS : (g + 1) * K_PASS, :]
            nc.sync.dma_start(raw[:], k_rows.rearrange("(p j) c -> p j c", j=PACK))
            return raw

        load_words(0)
        w1_raw = [load_weights(w1, "w1", 0, "w1_raw0")]
        load_words(1)

        xw = [keep.tile([P, S], U32, name="xw0", align_bytes=64)]
        xs_picked = keep.tile([P, S], U8, name="xs_picked", align_bytes=64)
        xs = []

        def scale_plane(g, on, shift):
            plane = place([P, S], U8, f"xs{g}", on, shift)
            nc.vector.memset(plane[:].bitcast(I32), 0)
            for q in range(QUADRANTS):
                row = rows_at + SCALE_ROWS * (QUADRANTS * g + q)
                nc.sync.dma_start(
                    plane[QUADRANT * q : QUADRANT * q + SCALE_ROWS, :].bitcast(I32),
                    xs_picked[row : row + SCALE_ROWS, :].bitcast(I32),
                )
            xs.append(plane)

        def pair_tile(name):
            if name in ("w1_00", "w1_01"):
                return place([P, PAIR, P, PACK], BF16, f"{name}_bf", "tile1_codes", 4096 + 2048 * int(name[-1]))
            return keep.tile([P, PAIR, P, PACK], BF16, name=f"{name}_bf", tag=f"{name}_bf", align_bytes=64)

        def deal_views(dealt, raw, pair, m0, m1):
            return (
                dealt[:, :, m0:m1, :].rearrange("p t m j -> p m j t"),
                raw[:].rearrange("p j (m t) -> p m j t", t=PACK)[:, m0:m1, :, PAIR * pair : PAIR * (pair + 1)],
            )

        def deal_on_scalar(dealt, raw, pair, m0=0, m1=P):
            nc.scalar.activation(*deal_views(dealt, raw, pair, m0, m1), ACT.Copy)

        def deal_on_vector(dealt, raw, pair, m0=0, m1=P):
            nc.vector.tensor_copy(*deal_views(dealt, raw, pair, m0, m1))

        def quantise_weights(dealt, name, tag=None):
            tiles = dealt.shape[1]
            if name in ("w1_10a", "w1_11"):
                codes = place([P, tiles * P], U32, f"{name}_codes", "tile1_codes")
            else:
                codes = keep.tile([P, tiles * P], U32, name=f"{name}_codes", tag=tag or f"{name}_codes", align_bytes=64)
            scales = keep.tile([P, tiles * P], U8, name=f"{name}_scales", align_bytes=64)
            nc.vector.quantize_mx(
                out=codes[:].bitcast(FP8X4), scales=scales[:], in_=dealt.rearrange("p t m j -> p (t m j)")
            )
            return [(codes[:, t * P : (t + 1) * P], scales[:, t * P : (t + 1) * P]) for t in range(tiles)]

        def product(w_passes, name, t, first_bank, emptiers, order=(0, 1), on=None):
            res = place([P, WINDOW], F32, f"{name}{t}", on)
            width = S // len(emptiers)
            for h, empty in enumerate(emptiers):
                cols = slice(h * width, (h + 1) * width)
                acc = psum.tile([P, width], F32, name="acc", tag=f"bank{first_bank + h}")
                for g in order:
                    codes, scales = w_passes[g][t]
                    nc.tensor.matmul_mx(
                        out=acc[:],
                        lhsT=codes.bitcast(FP8X4),
                        lhsT_scale=scales,
                        rhs=xw[g][:, cols].bitcast(FP8X4),
                        rhs_scale=xs[g][:, cols],
                        start=(g == order[0]),
                        stop=(g == order[-1]),
                    )
                empty(res[:, cols], acc[:])
            return res

        on_vector, on_scalar = nc.vector.tensor_copy, nc.scalar.copy

        nc.vector.tensor_copy(xs_picked[:], xs_all[:].indirect(offs_sb[:]))
        scale_plane(0, None, 0)
        nc.vector.tensor_copy(xw[0][:], xw_all[0][:].bitcast(U32).indirect(offs_sb[:]))
        w1_raw.append(load_weights(w1, "w1", 1, "w1_raw1"))
        scale_plane(1, None, 0)
        nc.sync.dma_start(src_sb[:], src)
        w1_00, w1_01, w1_10, w1_11 = [pair_tile(f"w1_{g}{pair}") for g in range(PASSES) for pair in range(2)]
        deal_on_scalar(w1_00, w1_raw[0], 0)
        deal_on_vector(w1_01, w1_raw[0], 1)
        w1_passes = [quantise_weights(w1_00[:], "w1_00") + quantise_weights(w1_01[:], "w1_01")]
        w2_raw = [load_weights(w2, "w2", 0, "w1_raw0", -64)]
        xw.append(place([P, S], U32, "xw1", "tile1_codes", 4096))
        nc.vector.tensor_copy(xw[1][:], xw_all[1][:].bitcast(U32).indirect(offs_sb[:]))
        w2_raw.append(load_weights(w2, "w2", 1, None))
        nc.sync.dma_start(dst_sb[:], dst)
        deal_on_scalar(w1_10, w1_raw[1], 0, 0, W1_LAST_ON_SCALAR)
        deal_on_vector(w1_10, w1_raw[1], 0, W1_LAST_ON_SCALAR, P)
        w1_passes.append(quantise_weights(w1_10[:, 0:1], "w1_10a") + quantise_weights(w1_10[:, 1:2], "w1_10b"))
        deal_on_scalar(w1_11, w1_raw[1], 1, 0, P // 2)

        deal_on_vector(w1_11, w1_raw[1], 1, P // 2, P)
        w3_codes = place([P, N], I32, "w3_codes")
        nc.sync.dma_start(w3_codes[:], w3_words[0].rearrange("p n j -> p (n j)").bitcast(I32))
        w3_plane = place([P, N], U8, "w3_plane")
        nc.vector.memset(w3_plane[:].bitcast(I32), 0)
        for q in range(QUADRANTS):
            nc.sync.dma_start(
                w3_plane[QUADRANT * q : QUADRANT * q + SCALE_ROWS, :].bitcast(I32),
                w3_scales[0, SCALE_ROWS * q : SCALE_ROWS * (q + 1), :].bitcast(I32),
            )

        area = keep.tile([P, PACK * S], F32, name="area")
        sums = area[:].rearrange("p (t r) -> p t r", t=PACK)
        last = S - QUARTER
        out_rows = out.rearrange("(h p) r -> p h r", p=P)
        row_tiles = N // P

        def fetch(got, y_t, r0):
            nc.scalar.activation(got, y_t[:].indirect(entries(src_sb, r0, got.shape[1])), ACT.Copy)
            return got

        def add(plane, e_t, r0, got):
            nc.vector.tensor_tensor(plane, e_t[:].indirect(entries(dst_sb, r0, plane.shape[1])), got, ALU.add)

        def relu(planes, name, vector):
            z_bf = keep.tile([P, planes.shape[2], PACK], BF16, name=name, align_bytes=64)
            woven = z_bf[:].rearrange("p (a i) t -> p a t i", i=LINE)
            planes = planes.rearrange("p t (a i) -> p a t i", i=LINE)
            if vector:
                nc.vector.tensor_scalar_max(woven, planes, 0.0)
            else:
                nc.scalar.activation(woven, planes, ACT.Relu)
            return z_bf

        def quantise_z(z_bf, r0):
            n = z_bf.shape[1]
            z_codes = keep.tile([P, n], U32, name=f"z_codes{r0}", align_bytes=64)
            z_scales = keep.tile([P, n], U8, name=f"z_scales{r0}", align_bytes=64)
            nc.vector.quantize_mx(
                out=z_codes[:].bitcast(FP8X4), scales=z_scales[:], in_=z_bf[:].rearrange("p r t -> p (r t)")
            )
            return z_codes, z_scales

        def finish(z_mx, r0, banks, emptiers, queues):
            z_codes, z_scales = z_mx
            n = z_codes.shape[1]
            per_bank = row_tiles // len(banks)
            staged = keep.tile([P, row_tiles, n], F32, name=f"staged{r0}")
            for b, bank in enumerate(banks):
                rows = slice(b * per_bank, (b + 1) * per_bank)
                res = psum.tile([P, per_bank, n], F32, name="res", tag=f"bank{bank}")
                for h in range(per_bank):
                    m_cols = slice((b * per_bank + h) * P, (b * per_bank + h + 1) * P)
                    nc.tensor.matmul_mx(
                        out=res[:, h, :],
                        lhsT=w3_codes[:, m_cols].bitcast(FP8X4),
                        lhsT_scale=w3_plane[:, m_cols],
                        rhs=z_codes[:].bitcast(FP8X4),
                        rhs_scale=z_scales[:],
                        start=True,
                        stop=True,
                    )
                emptiers[b](staged[:, rows, :], res[:])
                queues[b].dma_start(out_rows[:, rows, r0 : r0 + n], staged[:, rows, :])

        w2_01, w2_11 = pair_tile("w2_01"), pair_tile("w2_11")
        relay = keep.tile([P, S], F32, name="relay", align_bytes=64)
        w2_00, w2_10 = [
            half.bitcast(BF16).rearrange("p (t m j) -> p t m j", t=PAIR, j=PACK)
            for half in (relay[:, :HALF], relay[:, HALF:])
        ]
        y0 = product(w1_passes, "y", 0, 0, (on_vector, on_scalar, on_vector, on_scalar))
        ys0 = fetch(keep.tile([P, S], F32, name="ys0")[:], y0, 0)
        w1_passes[1].extend(quantise_weights(w1_11[:], "w1_11"))
        deal_on_vector(w2_00, w2_raw[0], 0)
        y1 = product(w1_passes, "y", 1, 4, (on_vector, on_scalar), on="y1")
        deal_on_vector(w2_01, w2_raw[0], 1)
        w2_passes = [quantise_weights(w2_00, "w2_00")]
        deal_on_vector(w2_10, w2_raw[1], 0)
        w2_passes[0].extend(quantise_weights(w2_01[:], "w2_01"))
        deal_on_vector(w2_11, w2_raw[1], 1)
        w2_passes.append(quantise_weights(w2_10, "w2_10") + quantise_weights(w2_11[:], "w2_11"))
        y2 = product(w1_passes, "y", 2, 6, (on_scalar, on_scalar))
        y3 = product(w1_passes, "y", 3, 0, (on_scalar, on_scalar))
        e0 = product(w2_passes, "e", 0, 2, (on_scalar, on_scalar))
        ys1 = relay[:]
        nc.vector.tensor_copy(ys1, y1[:].indirect(src_sb[:]))
        e1 = product(w2_passes, "e", 1, 4, (on_scalar, on_scalar))
        ys_early = place([P, S], F32, "ys_early", "y1")
        ys2_early = fetch(ys_early[:, :HALF], y2, 0)
        add(sums[:, 0, :], e0, 0, ys0)
        e2 = product(w2_passes, "e", 2, 6, (on_scalar, on_scalar), (1, 0))
        ys3_early = fetch(ys_early[:, HALF:], y3, 0)
        e3 = product(w2_passes, "e", 3, 0, (on_scalar, on_scalar), (1, 0))
        add(sums[:, 1, :], e1, 0, ys1)
        add(sums[:, 2, :HALF], e2, 0, ys2_early)
        add(sums[:, 3, :QUARTER], e3, 0, ys3_early[:, :QUARTER])
        add(sums[:, 3, QUARTER:HALF], e3, QUARTER, ys3_early[:, QUARTER:])
        ys2_late = fetch(relay[:, :HALF], y2, HALF)
        ys3_late = fetch(relay[:, HALF:], y3, HALF)
        z_a = relu(sums[:, :, :QUARTER], "z_a", True)
        z_b = relu(sums[:, :, QUARTER:HALF], "z_b", False)
        add(sums[:, 2, HALF:last], e2, HALF, ys2_late[:, :QUARTER])
        finish(quantise_z(z_a, 0), 0, (6,), (on_scalar,), (nc.sync,))
        add(sums[:, 2, last:], e2, last, ys2_late[:, QUARTER:])
        add(sums[:, 3, HALF:last], e3, HALF, ys3_late[:, :QUARTER])
        finish(quantise_z(z_b, QUARTER), QUARTER, (7,), (on_scalar,), (nc.sync,))
        eighth = QUARTER // 2
        add(sums[:, 3, last : last + eighth], e3, last, ys3_late[:, QUARTER : QUARTER + eighth])
        z_c = relu(sums[:, :, HALF:last], "z_c", True)
        z_d = relu(sums[:, :, last : last + eighth], "z_d", False)
        add(sums[:, 3, last + eighth :], e3, last + eighth, ys3_late[:, QUARTER + eighth :])
        finish(quantise_z(z_c, HALF), HALF, (4, 2), (on_scalar, on_scalar), (nc.sync, nc.sync))
        z_e = relu(sums[:, :, last + eighth :], "z_e", True)
        finish(quantise_z(z_d, last), last, (5,), (on_vector,), (nc.sync,))
        finish(quantise_z(z_e, last + eighth), last + eighth, (0, 1), (on_scalar, on_vector), (nc.scalar, nc.sync))
